import numpy as np
import ml_dtypes


def mxq(x, axis, fmt="e4m3"):
    dtype, down = {"e4m3": (ml_dtypes.float8_e4m3fn, 7), "e5m2": (ml_dtypes.float8_e5m2, 14)}[fmt]
    v = np.moveaxis(np.asarray(x, np.float32).astype(ml_dtypes.bfloat16).astype(np.float64), axis, -1)
    blocks = v.reshape(v.shape[:-1] + (-1, 32))
    amax = np.abs(blocks).max(-1, keepdims=True)
    byte = np.maximum(np.where(amax > 0, np.frexp(amax)[1] - 1 + 127, 0) - down, 1)
    scale = np.exp2(byte - 127.0)
    codes = (blocks / scale).astype(np.float32).astype(dtype).astype(np.float64)
    return np.moveaxis((codes * scale).reshape(v.shape), -1, axis)


WIDE = False


def mx_kscale(k):
    if not WIDE:
        return np.ones(k)
    levels = np.array([10, -10, 5, -5, 0])
    if k % 512:
        return np.exp2(np.random.permutation(np.resize(levels, k // 32))).repeat(32)
    a = np.empty((k // 512, 16))
    for p in range(k // 512):
        a[p, :8] = np.random.permutation(np.resize(levels, 8))
        for g in range(8):
            far = levels[np.abs(levels - a[p, g]) >= 10]
            a[p, g + 8] = far[np.random.randint(len(far))]
    return np.exp2(a.ravel()).repeat(32)


def f64(x):
    return np.asarray(x).astype(np.float64)


def striped(idx):
    return np.tile(idx.reshape(-1, 16).T, (8, 1)).astype(np.uint16)


def unstriped(offs):
    return offs[:16].T.reshape(-1).astype(np.int64)


E2M1 = np.array([0.0, 0.5, 1.0, 1.5, 2.0, 3.0, 4.0, 6.0, -0.0, -0.5, -1.0, -1.5, -2.0, -3.0, -4.0, -6.0])


def pack_weight(w, fmt):
    k, n = w.shape
    w = f64(np.asarray(w, np.float32).astype(ml_dtypes.bfloat16)).reshape(k // 32, 32, n)
    amax = np.abs(w).max(1)
    if fmt == "e4m3":
        byte = np.frexp(amax)[1] - 1 + 127 - 7
    else:
        mant, ex = np.frexp(amax / 6.0)
        byte = np.where(mant > 0.5, ex, ex - 1) + 127
    byte = np.clip(np.where(amax > 0, byte, 1), 1, 254)
    scaled = (w * np.exp2(127.0 - byte)[:, None, :]).reshape(k, n).astype(np.float32)
    by_word = np.ascontiguousarray(scaled.reshape(k // 512, 128, 4, n).transpose(0, 1, 3, 2))
    if fmt == "e4m3":
        words = by_word.astype(ml_dtypes.float8_e4m3fn).view(np.uint8)
    else:
        c = by_word.astype(ml_dtypes.float4_e2m1fn).view(np.uint8) & 0xF
        words = (c[..., 0::2] | (c[..., 1::2] << 4)).reshape(k // 512, 128, 2 * n)
    return np.ascontiguousarray(words), np.ascontiguousarray(byte.astype(np.uint8).reshape(k // 512, 16, n))


def unpack_weight(words, scales, fmt):
    g, _, n = scales.shape
    words = np.ascontiguousarray(words).reshape(g, 128, n, -1)
    if fmt == "e4m3":
        vals = words.view(ml_dtypes.float8_e4m3fn).astype(np.float64)
    else:
        nib = np.empty((g, 128, n, 4), np.uint8)
        nib[..., 0::2] = words & 0xF
        nib[..., 1::2] = words >> 4
        vals = E2M1[nib]
    vals = vals * np.repeat(np.exp2(scales.astype(np.float64) - 127.0), 8, axis=1)[..., None]
    return vals.transpose(0, 1, 3, 2).reshape(g * 512, n)


def silu(v):
    return v / (1.0 + np.exp(-np.maximum(v, -700.0)))


D, T, E, C, H, N, TOP = 3, 256, 18, 128, 512, 256, 3


def by_expert(wq, xq):
    return np.concatenate([wq[e].T @ xq[:, e * C:(e + 1) * C] for e in range(E)], axis=1)


def setup_inputs():
    n = np.random.standard_normal
    s = np.tile(mx_kscale(H), D)
    u = mx_kscale(H)
    X = D * T
    deal = np.repeat(np.arange(E), C).reshape(TOP, X)[:, np.random.permutation(X)]
    deal = np.take_along_axis(deal, np.argsort(np.random.rand(TOP, X), axis=0), axis=0)
    for _ in range(8):
        s_, t_ = np.random.permutation(X).reshape(2, -1); r = np.random.randint(TOP, size=X // 2); x, y = deal[r, s_].copy(), deal[r, t_].copy()
        ok = ~((deal[:, s_] == y).any(0) | (deal[:, t_] == x).any(0)); deal[r[ok], s_[ok]] = y[ok]; deal[r[ok], t_[ok]] = x[ok]
    order = np.lexsort((np.random.rand(TOP * X), deal.reshape(-1)))
    slot_sub = order % X; pos = np.empty(TOP * X, np.int64); pos[order] = np.arange(TOP * X); pos = pos.reshape(TOP, X)
    g = np.random.uniform(0.5, 1.5, (TOP, X)); g = g / g.sum(0)
    x = pack_weight(n((D * H, T)) * s[:, None], "e4m3")
    w = [pack_weight(m, "e2m1") for m in n((E, H, H)) / np.sqrt(H) / s[None, :H, None] * u]
    wm = pack_weight(n((D * H, N)) / np.sqrt(D * H) / np.tile(u, D)[:, None], "e2m1")
    return {
        "x_words": x[0],
        "x_scales": x[1],
        "w_words": np.stack([m[0] for m in w]),
        "w_scales": np.stack([m[1] for m in w]),
        "wm_words": wm[0],
        "wm_scales": wm[1],
        "gate": np.stack([np.tile(r, (128, 1)) for r in g]).astype(np.float32),
        "offs": striped(slot_sub),
        "pos1": striped(pos[0]),
        "pos2": striped(pos[1]),
        "pos3": striped(pos[2]),
    }


def reference(x_words, x_scales, w_words, w_scales, wm_words, wm_scales, gate, offs, pos1, pos2, pos3):
    w = np.stack([unpack_weight(w_words[e], w_scales[e], "e2m1") for e in range(E)])
    wm = unpack_weight(wm_words, wm_scales, "e2m1")
    idx = unstriped(offs)
    x = unpack_weight(x_words, x_scales, "e4m3")
    sub = x.reshape(D, H, T).transpose(1, 0, 2).reshape(H, D * T)
    y = silu(by_expert(w, sub[:, idx]))
    c = sum(f64(gate[r, :1]) * y[:, unstriped(p)] for r, p in enumerate((pos1, pos2, pos3)))
    cq = mxq(c, 0, "e4m3").reshape(H, D, T).transpose(1, 0, 2).reshape(D * H, T)
    return wm.T @ cq

@@ -1,0 +1,201 @@
+from contextlib import ExitStack
+
+import concourse.mybir as mybir
+from concourse.masks import make_identity
+
+HEADS, T, E, C, H, N, TOP = 3, 256, 18, 128, 512, 256, 3
+Z = HEADS * T
+S = E * C
+FLOPS = 2 * H * H * S + 2 * HEADS * H * N * T
+
+F32 = mybir.dt.float32
+BF16 = mybir.dt.bfloat16
+I32 = mybir.dt.int32
+U32 = mybir.dt.uint32
+U16 = mybir.dt.uint16
+U8 = mybir.dt.uint8
+FP8X4 = mybir.dt.float8_e4m3fn_x4
+FP4X4 = mybir.dt.float4_e2m1fn_x4
+MULT = mybir.AluOpType.mult
+SILU = mybir.ActivationFunctionType.Silu
+
+P = 128
+L_TILES = H // P
+BANK = 512
+LIST_COL = 16
+EXPERT_GROUPS = [(0, 4), (4, 8), (8, 12), (12, 16), (16, 18)]
+WORD_LOADS = [(0, 4), (4, 9), (9, 14), (14, 18)]
+LAST_PIECES = [(0, 256), (256, 512), (512, 640), (640, 768)]
+
+
+def load_scale_rows(nc, plane, rows):
+    for q in range(4):
+        nc.sync.dma_start(
+            out=plane[32 * q : 32 * q + 4].bitcast(I32),
+            in_=rows[:, 4 * q : 4 * q + 4, :].rearrange("a b n -> b a n").bitcast(I32),
+        )
+
+
+def tile_moe_mhm_silu_kernel(
+    tc, x_words, x_scales, w_words, w_scales, wm_words, wm_scales, gate, offs, pos1, pos2, pos3, out
+):
+    nc = tc.nc
+    with ExitStack() as ctx:
+        keep = ctx.enter_context(tc.tile_pool(name="keep", bufs=1))
+        ring = ctx.enter_context(tc.tile_pool(name="ring", bufs=2))
+        psum = ctx.enter_context(tc.psum_pool(name="psum", bufs=2))
+
+        slot_list = keep.tile([P, S // LIST_COL], U16, name="slot_list")
+        pos = [keep.tile([P, Z // LIST_COL], U16, name="pos%d" % r) for r in range(TOP)]
+        xw = keep.tile([P, Z], I32, name="xw", align_bytes=64)
+        xs = keep.tile([P, Z], U8, name="xs", align_bytes=64)
+        ww = keep.tile([P, E, 2 * H], U8, name="ww", align_bytes=64)
+        ws = keep.tile([P, E, H], U8, name="ws", align_bytes=64)
+        mw = keep.tile([P, HEADS, 2 * N], U8, name="mw", align_bytes=64)
+        ms = keep.tile([P, HEADS, N], U8, name="ms", align_bytes=64)
+        gates = [keep.tile([P, Z], F32, name="gate%d" % r) for r in range(TOP)]
+        y = [keep.tile([P, S], F32, name="y%d" % j) for j in range(L_TILES)]
+        c_rows = keep.tile([P, Z // P, H], BF16, name="c_rows", align_bytes=64)
+        ident = keep.tile([P, P], F32, name="ident")
+
+        nc.gpsimd.memset(xs[:].bitcast(I32), 0)
+        nc.vector.memset(ws[:].bitcast(I32), 0)
+        nc.vector.memset(ms[:].bitcast(I32), 0)
+        make_identity(nc, ident[:])
+
+        w_words_pe = w_words.rearrange("e s p c -> p (e s) c")
+
+        def load_words(e0, e1):
+            nc.sync.dma_start(out=ww[:, e0:e1, :].bitcast(I32), in_=w_words_pe[:, e0:e1, :].bitcast(I32))
+
+        nc.sync.dma_start(slot_list[:], offs)
+        nc.sync.dma_start(
+            out=xw[:].rearrange("p (o t) -> p o t", o=HEADS),
+            in_=x_words.rearrange("o p t d -> p o (t d)").bitcast(I32),
+        )
+        load_scale_rows(nc, xs[:].rearrange("p (o t) -> p o t", o=HEADS), x_scales)
+        for r, pos_r in enumerate((pos1, pos2, pos3)):
+            nc.sync.dma_start(pos[r][:], pos_r)
+        load_scale_rows(nc, ws[:], w_scales.rearrange("e s b l -> (e s) b l"))
+        for e0, e1 in WORD_LOADS:
+            load_words(e0, e1)
+        for r in range(TOP):
+            nc.sync.dma_start(out=gates[r][:], in_=gate[r])
+        nc.sync.dma_start(out=mw[:].bitcast(I32), in_=wm_words.rearrange("o p c -> p o c").bitcast(I32))
+        load_scale_rows(nc, ms[:], wm_scales)
+
+        slot_words, slot_scales = [], []
+        for g, (e0, e1) in enumerate(EXPERT_GROUPS):
+            width = (e1 - e0) * C
+            offsets = slot_list[:, e0 * C // LIST_COL : e1 * C // LIST_COL]
+            words = keep.tile([P, width], U32, name="slot_words%d" % g, align_bytes=64)
+            scales = keep.tile([P, width], U8, name="slot_scales%d" % g, align_bytes=64)
+            nc.vector.tensor_copy(words[:], xw[:].bitcast(U32).indirect(offsets))
+            nc.vector.tensor_copy(scales[:], xs[:].indirect(offsets))
+            slot_words.append(words)
+            slot_scales.append(scales)
+
+        def experts(j):
+            for g, (e0, e1) in enumerate(EXPERT_GROUPS):
+                if j == 0:
+                    bank = psum.tile([P, BANK], F32, name="bank", tag="sum", bufs=2)
+                else:
+                    bank = psum.tile([P, BANK], F32, name="bank", tag="mx", bufs=4)
+                for e in range(e0, e1):
+                    cols = slice((e - e0) * C, (e - e0 + 1) * C)
+                    nc.tensor.matmul_mx(
+                        out=bank[:, cols],
+                        lhsT=ww[:, e, 2 * P * j : 2 * P * (j + 1)].bitcast(FP4X4),
+                        lhsT_scale=ws[:, e, P * j : P * (j + 1)],
+                        rhs=slot_words[g][:, cols].bitcast(FP8X4),
+                        rhs_scale=slot_scales[g][:, cols],
+                        start=True,
+                        stop=True,
+                    )
+                nc.scalar.activation(y[j][:, e0 * C : e1 * C], bank[:, : (e1 - e0) * C], SILU)
+
+        def gather(j, z0, z1):
+            terms = []
+            for r in range(TOP):
+                term = ring.tile([P, z1 - z0], F32, name="term", tag="term%d" % r)
+                offsets = pos[r][:, z0 // LIST_COL : z1 // LIST_COL]
+                nc.vector.tensor_tensor(term[:], y[j][:].indirect(offsets), gates[r][:, z0:z1], MULT)
+                terms.append(term)
+            return terms
+
+        def add_turned(j, terms, z0, b0, b1, copy):
+            bank = psum.tile([P, b1 - b0, P], F32, name="bank", tag="sum", bufs=2)
+            for b in range(b0, b1):
+                for r in range(TOP):
+                    nc.tensor.matmul(
+                        bank[:, b - b0, :],
+                        terms[r][:, b * P - z0 : (b + 1) * P - z0],
+                        ident[:],
+                        start=(r == 0),
+                        stop=(r == TOP - 1),
+                        is_transpose=True,
+                    )
+            copy(c_rows[:, b0:b1, P * j : P * (j + 1)], bank[:])
+
+        def turn_back(z0, z1):
+            blocks = (z1 - z0) // P
+            bank = psum.tile([P, blocks, 2, P], F32, name="bank", tag="back", bufs=2)
+            for b in range(blocks):
+                pairs = c_rows[:, z0 // P + b, :].bitcast(F32)
+                for u in range(2):
+                    nc.tensor.transpose(bank[:, b, u, :], pairs[:, u : H // 2 : 2], ident[:])
+            grouped = keep.tile([P, 4 * (z1 - z0)], BF16, name="grouped%d" % z0, align_bytes=64)
+            nc.scalar.copy(
+                grouped[:].bitcast(F32).rearrange("p (b z u) -> p b z u", b=blocks, u=2),
+                bank[:].rearrange("p b u z -> p b z u"),
+            )
+            return grouped
+
+        def merge(grouped, z0, z1, sums):
+            codes = keep.tile([P, z1 - z0], U32, name="c_codes%d" % z0, align_bytes=64)
+            scales = keep.tile([P, z1 - z0], U8, name="c_scales%d" % z0, align_bytes=64)
+            nc.vector.quantize_mx(out=codes[:].bitcast(FP8X4), scales=scales[:], in_=grouped[:])
+            for b in range(z0 // P, z1 // P):
+                o, th = divmod(b, T // P)
+                cols = slice(b * P - z0, (b + 1) * P - z0)
+                for nh in range(N // P):
+                    nc.tensor.matmul_mx(
+                        out=sums[th][nh][:],
+                        lhsT=mw[:, o, 2 * P * nh : 2 * P * (nh + 1)].bitcast(FP4X4),
+                        lhsT_scale=ms[:, o, P * nh : P * (nh + 1)],
+                        rhs=codes[:, cols].bitcast(FP8X4),
+                        rhs_scale=scales[:, cols],
+                        start=(o == 0),
+                        stop=(o == HEADS - 1),
+                    )
+                if o == HEADS - 1:
+                    for nh in range(N // P):
+                        result = ring.tile([P, P], F32, name="result", tag="result%d" % nh)
+                        dest = out[nh * P : (nh + 1) * P, th * P : (th + 1) * P]
+                        if nh == 0:
+                            nc.scalar.copy(result[:], sums[th][nh][:])
+                            nc.scalar.dma_start(out=dest, in_=result[:])
+                        else:
+                            nc.vector.tensor_copy(result[:], sums[th][nh][:])
+                            nc.sync.dma_start(out=dest, in_=result[:])
+
+        for j in range(L_TILES):
+            experts(j)
+
+        for j in range(L_TILES - 1):
+            terms = gather(j, 0, Z)
+            add_turned(j, terms, 0, 0, 3, nc.scalar.copy)
+            add_turned(j, terms, 0, 3, 6, nc.scalar.copy)
+
+        sums = [
+            [psum.tile([P, P], F32, name="sums", tag="mx", bufs=4) for nh in range(N // P)]
+            for th in range(T // P)
+        ]
+        grouped = []
+        for z0, z1 in LAST_PIECES:
+            terms = gather(L_TILES - 1, z0, z1)
+            copy = nc.vector.tensor_copy if z1 == Z else nc.scalar.copy
+            add_turned(L_TILES - 1, terms, z0, z0 // P, z1 // P, copy)
+            grouped.append(turn_back(z0, z1))
+        for piece, (z0, z1) in zip(grouped, LAST_PIECES):
+            merge(piece, z0, z1, sums)

@@ -24,8 +24,8 @@ L_TILES = H // P
 BANK = 512
 LIST_COL = 16
 EXPERT_GROUPS = [(0, 4), (4, 8), (8, 12), (12, 16), (16, 18)]
-WORD_LOADS = [(0, 4), (4, 9), (9, 14), (14, 18)]
-LAST_PIECES = [(0, 256), (256, 512), (512, 640), (640, 768)]
+WORD_LOADS = [(0, 6), (6, 12), (12, 18)]
+LAST_PIECES = [(0, 256), (256, 384), (384, 512), (512, 640), (640, 768)]
 
 
 def load_scale_rows(nc, plane, rows):
@@ -42,31 +42,42 @@ def tile_moe_mhm_silu_kernel(
     nc = tc.nc
     with ExitStack() as ctx:
         keep = ctx.enter_context(tc.tile_pool(name="keep", bufs=1))
-        ring = ctx.enter_context(tc.tile_pool(name="ring", bufs=2))
-        psum = ctx.enter_context(tc.psum_pool(name="psum", bufs=2))
+        ring = ctx.enter_context(tc.tile_pool(name="ring", bufs=3))
+        psum = ctx.enter_context(tc.psum_pool(name="psum", bufs=1))
 
         slot_list = keep.tile([P, S // LIST_COL], U16, name="slot_list")
         pos = [keep.tile([P, Z // LIST_COL], U16, name="pos%d" % r) for r in range(TOP)]
         xw = keep.tile([P, Z], I32, name="xw", align_bytes=64)
         xs = keep.tile([P, Z], U8, name="xs", align_bytes=64)
-        ww = keep.tile([P, E, 2 * H], U8, name="ww", align_bytes=64)
-        ws = keep.tile([P, E, H], U8, name="ws", align_bytes=64)
+        ww = [keep.tile([P, E, H], U8, name="ww%d" % h, align_bytes=64) for h in range(2)]
+        ws = [keep.tile([P, E, H // 2], U8, name="ws%d" % h, align_bytes=64) for h in range(2)]
         mw = keep.tile([P, HEADS, 2 * N], U8, name="mw", align_bytes=64)
         ms = keep.tile([P, HEADS, N], U8, name="ms", align_bytes=64)
         gates = [keep.tile([P, Z], F32, name="gate%d" % r) for r in range(TOP)]
         y = [keep.tile([P, S], F32, name="y%d" % j) for j in range(L_TILES)]
-        c_rows = keep.tile([P, Z // P, H], BF16, name="c_rows", align_bytes=64)
+        c_rows = keep.tile([P, Z // P, 2, P, 2], BF16, name="c_rows", align_bytes=64)
         ident = keep.tile([P, P], F32, name="ident")
 
+        banks = [psum.tile([P, BANK], F32, name="bank%d" % b) for b in range(8)]
+        expert_banks, sum_banks, merge_banks, back_banks = banks[0:6], banks[0:2], banks[2:6], banks[6:8]
+
         nc.gpsimd.memset(xs[:].bitcast(I32), 0)
-        nc.vector.memset(ws[:].bitcast(I32), 0)
+        for h in range(2):
+            nc.vector.memset(ws[h][:].bitcast(I32), 0)
         nc.vector.memset(ms[:].bitcast(I32), 0)
         make_identity(nc, ident[:])
 
         w_words_pe = w_words.rearrange("e s p c -> p (e s) c")
 
-        def load_words(e0, e1):
-            nc.sync.dma_start(out=ww[:, e0:e1, :].bitcast(I32), in_=w_words_pe[:, e0:e1, :].bitcast(I32))
+        w_scales_eb = w_scales.rearrange("e s b l -> (e s) b l")
+
+        def load_w_half(h):
+            load_scale_rows(nc, ws[h][:], w_scales_eb[:, :, h * H // 2 : (h + 1) * H // 2])
+            for e0, e1 in WORD_LOADS:
+                nc.sync.dma_start(
+                    out=ww[h][:, e0:e1, :].bitcast(I32),
+                    in_=w_words_pe[:, e0:e1, h * H : (h + 1) * H].bitcast(I32),
+                )
 
         nc.sync.dma_start(slot_list[:], offs)
         nc.sync.dma_start(
@@ -76,11 +87,10 @@ def tile_moe_mhm_silu_kernel(
         load_scale_rows(nc, xs[:].rearrange("p (o t) -> p o t", o=HEADS), x_scales)
         for r, pos_r in enumerate((pos1, pos2, pos3)):
             nc.sync.dma_start(pos[r][:], pos_r)
-        load_scale_rows(nc, ws[:], w_scales.rearrange("e s b l -> (e s) b l"))
-        for e0, e1 in WORD_LOADS:
-            load_words(e0, e1)
+        load_w_half(0)
         for r in range(TOP):
             nc.sync.dma_start(out=gates[r][:], in_=gate[r])
+        load_w_half(1)
         nc.sync.dma_start(out=mw[:].bitcast(I32), in_=wm_words.rearrange("o p c -> p o c").bitcast(I32))
         load_scale_rows(nc, ms[:], wm_scales)
 
@@ -95,24 +105,20 @@ def tile_moe_mhm_silu_kernel(
             slot_words.append(words)
             slot_scales.append(scales)
 
-        def experts(j):
-            for g, (e0, e1) in enumerate(EXPERT_GROUPS):
-                if j == 0:
-                    bank = psum.tile([P, BANK], F32, name="bank", tag="sum", bufs=2)
-                else:
-                    bank = psum.tile([P, BANK], F32, name="bank", tag="mx", bufs=4)
-                for e in range(e0, e1):
-                    cols = slice((e - e0) * C, (e - e0 + 1) * C)
-                    nc.tensor.matmul_mx(
-                        out=bank[:, cols],
-                        lhsT=ww[:, e, 2 * P * j : 2 * P * (j + 1)].bitcast(FP4X4),
-                        lhsT_scale=ws[:, e, P * j : P * (j + 1)],
-                        rhs=slot_words[g][:, cols].bitcast(FP8X4),
-                        rhs_scale=slot_scales[g][:, cols],
-                        start=True,
-                        stop=True,
-                    )
-                nc.scalar.activation(y[j][:, e0 * C : e1 * C], bank[:, : (e1 - e0) * C], SILU)
+        def experts(j, g, bank):
+            e0, e1 = EXPERT_GROUPS[g]
+            for e in range(e0, e1):
+                cols = slice((e - e0) * C, (e - e0 + 1) * C)
+                nc.tensor.matmul_mx(
+                    out=bank[:, cols],
+                    lhsT=ww[j // 2][:, e, 2 * P * (j % 2) : 2 * P * (j % 2 + 1)].bitcast(FP4X4),
+                    lhsT_scale=ws[j // 2][:, e, P * (j % 2) : P * (j % 2 + 1)],
+                    rhs=slot_words[g][:, cols].bitcast(FP8X4),
+                    rhs_scale=slot_scales[g][:, cols],
+                    start=True,
+                    stop=True,
+                )
+            nc.scalar.activation(y[j][:, e0 * C : e1 * C], bank[:, : (e1 - e0) * C], SILU)
 
         def gather(j, z0, z1):
             terms = []
@@ -123,8 +129,8 @@ def tile_moe_mhm_silu_kernel(
                 terms.append(term)
             return terms
 
-        def add_turned(j, terms, z0, b0, b1, copy):
-            bank = psum.tile([P, b1 - b0, P], F32, name="bank", tag="sum", bufs=2)
+        def add_turned(j, terms, z0, b0, b1, copy, bank):
+            bank = bank[:, : (b1 - b0) * P].rearrange("p (b l) -> p b l", l=P)
             for b in range(b0, b1):
                 for r in range(TOP):
                     nc.tensor.matmul(
@@ -135,19 +141,23 @@ def tile_moe_mhm_silu_kernel(
                         stop=(r == TOP - 1),
                         is_transpose=True,
                     )
-            copy(c_rows[:, b0:b1, P * j : P * (j + 1)], bank[:])
+            for b in range(b0, b1):
+                copy(
+                    c_rows[:, b, :, 32 * j : 32 * (j + 1), :],
+                    bank[:, b - b0, :].rearrange("z (q u e) -> z u q e", u=2, e=2),
+                )
 
-        def turn_back(z0, z1):
+        def turn_back(z0, z1, bank):
             blocks = (z1 - z0) // P
-            bank = psum.tile([P, blocks, 2, P], F32, name="bank", tag="back", bufs=2)
+            bank = bank[:, : blocks * 2 * P].rearrange("p (b u z) -> p b u z", u=2, z=P)
             for b in range(blocks):
-                pairs = c_rows[:, z0 // P + b, :].bitcast(F32)
                 for u in range(2):
-                    nc.tensor.transpose(bank[:, b, u, :], pairs[:, u : H // 2 : 2], ident[:])
+                    pairs = c_rows[:, z0 // P + b, u, :, :].rearrange("z p e -> z (p e)").bitcast(F32)
+                    nc.tensor.transpose(bank[:, b, u, :], pairs, ident[:])
             grouped = keep.tile([P, 4 * (z1 - z0)], BF16, name="grouped%d" % z0, align_bytes=64)
             nc.scalar.copy(
                 grouped[:].bitcast(F32).rearrange("p (b z u) -> p b z u", b=blocks, u=2),
-                bank[:].rearrange("p b u z -> p b z u"),
+                bank.rearrange("p b u z -> p b z u"),
             )
             return grouped
 
@@ -160,7 +170,7 @@ def tile_moe_mhm_silu_kernel(
                 cols = slice(b * P - z0, (b + 1) * P - z0)
                 for nh in range(N // P):
                     nc.tensor.matmul_mx(
-                        out=sums[th][nh][:],
+                        out=sums[th][nh],
                         lhsT=mw[:, o, 2 * P * nh : 2 * P * (nh + 1)].bitcast(FP4X4),
                         lhsT_scale=ms[:, o, P * nh : P * (nh + 1)],
                         rhs=codes[:, cols].bitcast(FP8X4),
@@ -173,29 +183,28 @@ def tile_moe_mhm_silu_kernel(
                         result = ring.tile([P, P], F32, name="result", tag="result%d" % nh)
                         dest = out[nh * P : (nh + 1) * P, th * P : (th + 1) * P]
                         if nh == 0:
-                            nc.scalar.copy(result[:], sums[th][nh][:])
+                            nc.scalar.copy(result[:], sums[th][nh])
                             nc.scalar.dma_start(out=dest, in_=result[:])
                         else:
-                            nc.vector.tensor_copy(result[:], sums[th][nh][:])
+                            nc.vector.tensor_copy(result[:], sums[th][nh])
                             nc.sync.dma_start(out=dest, in_=result[:])
 
-        for j in range(L_TILES):
-            experts(j)
+        order = [(0, 0), (0, 1), (1, 0), (0, 2), (1, 1), (0, 3), (0, 4), (1, 2), (1, 3), (1, 4)]
+        order += [(j, g) for j in range(2, L_TILES) for g in range(len(EXPERT_GROUPS))]
+        for i, (j, g) in enumerate(order):
+            experts(j, g, expert_banks[i % len(expert_banks)])
 
         for j in range(L_TILES - 1):
             terms = gather(j, 0, Z)
-            add_turned(j, terms, 0, 0, 3, nc.scalar.copy)
-            add_turned(j, terms, 0, 3, 6, nc.scalar.copy)
+            add_turned(j, terms, 0, 0, 3, nc.scalar.copy, sum_banks[0])
+            add_turned(j, terms, 0, 3, 6, nc.scalar.copy, sum_banks[1])
 
-        sums = [
-            [psum.tile([P, P], F32, name="sums", tag="mx", bufs=4) for nh in range(N // P)]
-            for th in range(T // P)
-        ]
+        sums = [[merge_banks[2 * th + nh][:, :P] for nh in range(N // P)] for th in range(T // P)]
         grouped = []
-        for z0, z1 in LAST_PIECES:
+        for i, (z0, z1) in enumerate(LAST_PIECES):
             terms = gather(L_TILES - 1, z0, z1)
             copy = nc.vector.tensor_copy if z1 == Z else nc.scalar.copy
-            add_turned(L_TILES - 1, terms, z0, z0 // P, z1 // P, copy)
-            grouped.append(turn_back(z0, z1))
+            add_turned(L_TILES - 1, terms, z0, z0 // P, z1 // P, copy, sum_banks[i % 2])
+            grouped.append(turn_back(z0, z1, back_banks[i % 2]))
         for piece, (z0, z1) in zip(grouped, LAST_PIECES):
             merge(piece, z0, z1, sums)

@@ -23,7 +23,7 @@ P = 128
 L_TILES = H // P
 BANK = 512
 LIST_COL = 16
-EXPERT_GROUPS = [(0, 4), (4, 8), (8, 12), (12, 16), (16, 18)]
+EXPERT_GROUPS = [(0, 4), (4, 8), (8, 12), (12, 15), (15, 17), (17, 18)]
 WORD_LOADS = [(0, 6), (6, 12), (12, 18)]
 LAST_PIECES = [(0, 256), (256, 384), (384, 512), (512, 640), (640, 768)]
 
@@ -48,7 +48,7 @@ def tile_moe_mhm_silu_kernel(
         slot_list = keep.tile([P, S // LIST_COL], U16, name="slot_list")
         pos = [keep.tile([P, Z // LIST_COL], U16, name="pos%d" % r) for r in range(TOP)]
         xw = keep.tile([P, Z], I32, name="xw", align_bytes=64)
-        xs = keep.tile([P, Z], U8, name="xs", align_bytes=64)
+        xs = keep.tile([P, 2 * Z], U8, name="xs", align_bytes=64)
         ww = [keep.tile([P, E, H], U8, name="ww%d" % h, align_bytes=64) for h in range(2)]
         ws = [keep.tile([P, E, H // 2], U8, name="ws%d" % h, align_bytes=64) for h in range(2)]
         mw = keep.tile([P, HEADS, 2 * N], U8, name="mw", align_bytes=64)
@@ -59,9 +59,11 @@ def tile_moe_mhm_silu_kernel(
         ident = keep.tile([P, P], F32, name="ident")
 
         banks = [psum.tile([P, BANK], F32, name="bank%d" % b) for b in range(8)]
-        expert_banks, sum_banks, merge_banks, back_banks = banks[0:6], banks[0:2], banks[2:6], banks[6:8]
+        expert_banks, sum_banks, back_banks = banks[0:6], banks[4:6], banks[6:8]
+        last_sum_bank, early_bank = banks[0], banks[1]
 
-        nc.gpsimd.memset(xs[:].bitcast(I32), 0)
+        nc.gpsimd.memset(xs[:, :Z].bitcast(I32), 0)
+        nc.gpsimd.memset(xs[:, Z:].bitcast(I32), 0)
         for h in range(2):
             nc.vector.memset(ws[h][:].bitcast(I32), 0)
         nc.vector.memset(ms[:].bitcast(I32), 0)
@@ -80,13 +82,13 @@ def tile_moe_mhm_silu_kernel(
                 )
 
         nc.sync.dma_start(slot_list[:], offs)
+        load_scale_rows(nc, xs[:, :Z].rearrange("p (o t) -> p o t", o=HEADS), x_scales)
+        for r, pos_r in enumerate((pos1, pos2, pos3)):
+            nc.sync.dma_start(pos[r][:], pos_r)
         nc.sync.dma_start(
             out=xw[:].rearrange("p (o t) -> p o t", o=HEADS),
             in_=x_words.rearrange("o p t d -> p o (t d)").bitcast(I32),
         )
-        load_scale_rows(nc, xs[:].rearrange("p (o t) -> p o t", o=HEADS), x_scales)
-        for r, pos_r in enumerate((pos1, pos2, pos3)):
-            nc.sync.dma_start(pos[r][:], pos_r)
         load_w_half(0)
         for r in range(TOP):
             nc.sync.dma_start(out=gates[r][:], in_=gate[r])
@@ -94,16 +96,14 @@ def tile_moe_mhm_silu_kernel(
         nc.sync.dma_start(out=mw[:].bitcast(I32), in_=wm_words.rearrange("o p c -> p o c").bitcast(I32))
         load_scale_rows(nc, ms[:], wm_scales)
 
-        slot_words, slot_scales = [], []
-        for g, (e0, e1) in enumerate(EXPERT_GROUPS):
-            width = (e1 - e0) * C
+        slot_scales = keep.tile([P, S], U8, name="slot_scales", align_bytes=64)
+        for s0 in range(0, S, S // 2):
+            offsets = slot_list[:, s0 // LIST_COL : (s0 + S // 2) // LIST_COL]
+            nc.vector.tensor_copy(slot_scales[:, s0 : s0 + S // 2], xs[:].indirect(offsets))
+        slot_words = keep.tile([P, S], U32, name="slot_words", align_bytes=64)
+        for e0, e1 in EXPERT_GROUPS:
             offsets = slot_list[:, e0 * C // LIST_COL : e1 * C // LIST_COL]
-            words = keep.tile([P, width], U32, name="slot_words%d" % g, align_bytes=64)
-            scales = keep.tile([P, width], U8, name="slot_scales%d" % g, align_bytes=64)
-            nc.vector.tensor_copy(words[:], xw[:].bitcast(U32).indirect(offsets))
-            nc.vector.tensor_copy(scales[:], xs[:].indirect(offsets))
-            slot_words.append(words)
-            slot_scales.append(scales)
+            nc.vector.tensor_copy(slot_words[:, e0 * C : e1 * C], xw[:].bitcast(U32).indirect(offsets))
 
         def experts(j, g, bank):
             e0, e1 = EXPERT_GROUPS[g]
@@ -113,8 +113,8 @@ def tile_moe_mhm_silu_kernel(
                     out=bank[:, cols],
                     lhsT=ww[j // 2][:, e, 2 * P * (j % 2) : 2 * P * (j % 2 + 1)].bitcast(FP4X4),
                     lhsT_scale=ws[j // 2][:, e, P * (j % 2) : P * (j % 2 + 1)],
-                    rhs=slot_words[g][:, cols].bitcast(FP8X4),
-                    rhs_scale=slot_scales[g][:, cols],
+                    rhs=slot_words[:, e * C : (e + 1) * C].bitcast(FP8X4),
+                    rhs_scale=slot_scales[:, e * C : (e + 1) * C],
                     start=True,
                     stop=True,
                 )
@@ -129,7 +129,7 @@ def tile_moe_mhm_silu_kernel(
                 terms.append(term)
             return terms
 
-        def add_turned(j, terms, z0, b0, b1, copy, bank):
+        def add_turned(j, terms, z0, b0, b1, bank):
             bank = bank[:, : (b1 - b0) * P].rearrange("p (b l) -> p b l", l=P)
             for b in range(b0, b1):
                 for r in range(TOP):
@@ -142,12 +142,12 @@ def tile_moe_mhm_silu_kernel(
                         is_transpose=True,
                     )
             for b in range(b0, b1):
-                copy(
+                nc.scalar.copy(
                     c_rows[:, b, :, 32 * j : 32 * (j + 1), :],
                     bank[:, b - b0, :].rearrange("z (q u e) -> z u q e", u=2, e=2),
                 )
 
-        def turn_back(z0, z1, bank):
+        def turn_back(z0, z1, bank, copy):
             blocks = (z1 - z0) // P
             bank = bank[:, : blocks * 2 * P].rearrange("p (b u z) -> p b u z", u=2, z=P)
             for b in range(blocks):
@@ -155,56 +155,61 @@ def tile_moe_mhm_silu_kernel(
                     pairs = c_rows[:, z0 // P + b, u, :, :].rearrange("z p e -> z (p e)").bitcast(F32)
                     nc.tensor.transpose(bank[:, b, u, :], pairs, ident[:])
             grouped = keep.tile([P, 4 * (z1 - z0)], BF16, name="grouped%d" % z0, align_bytes=64)
-            nc.scalar.copy(
+            copy(
                 grouped[:].bitcast(F32).rearrange("p (b z u) -> p b z u", b=blocks, u=2),
                 bank.rearrange("p b u z -> p b z u"),
             )
             return grouped
 
-        def merge(grouped, z0, z1, sums):
-            codes = keep.tile([P, z1 - z0], U32, name="c_codes%d" % z0, align_bytes=64)
-            scales = keep.tile([P, z1 - z0], U8, name="c_scales%d" % z0, align_bytes=64)
-            nc.vector.quantize_mx(out=codes[:].bitcast(FP8X4), scales=scales[:], in_=grouped[:])
-            for b in range(z0 // P, z1 // P):
-                o, th = divmod(b, T // P)
-                cols = slice(b * P - z0, (b + 1) * P - z0)
-                for nh in range(N // P):
-                    nc.tensor.matmul_mx(
-                        out=sums[th][nh],
-                        lhsT=mw[:, o, 2 * P * nh : 2 * P * (nh + 1)].bitcast(FP4X4),
-                        lhsT_scale=ms[:, o, P * nh : P * (nh + 1)],
-                        rhs=codes[:, cols].bitcast(FP8X4),
-                        rhs_scale=scales[:, cols],
-                        start=(o == 0),
-                        stop=(o == HEADS - 1),
-                    )
-                if o == HEADS - 1:
-                    for nh in range(N // P):
-                        result = ring.tile([P, P], F32, name="result", tag="result%d" % nh)
-                        dest = out[nh * P : (nh + 1) * P, th * P : (th + 1) * P]
-                        if nh == 0:
-                            nc.scalar.copy(result[:], sums[th][nh])
-                            nc.scalar.dma_start(out=dest, in_=result[:])
-                        else:
-                            nc.vector.tensor_copy(result[:], sums[th][nh])
-                            nc.sync.dma_start(out=dest, in_=result[:])
+        c_codes = keep.tile([P, Z], U32, name="c_codes", align_bytes=64)
+        c_scales = keep.tile([P, Z], U8, name="c_scales", align_bytes=64)
 
-        order = [(0, 0), (0, 1), (1, 0), (0, 2), (1, 1), (0, 3), (0, 4), (1, 2), (1, 3), (1, 4)]
-        order += [(j, g) for j in range(2, L_TILES) for g in range(len(EXPERT_GROUPS))]
+        def merge(sums, nh, th, o, start, stop):
+            cols = slice(o * T + th * P, o * T + (th + 1) * P)
+            nc.tensor.matmul_mx(
+                out=sums,
+                lhsT=mw[:, o, 2 * P * nh : 2 * P * (nh + 1)].bitcast(FP4X4),
+                lhsT_scale=ms[:, o, P * nh : P * (nh + 1)],
+                rhs=c_codes[:, cols].bitcast(FP8X4),
+                rhs_scale=c_scales[:, cols],
+                start=start,
+                stop=stop,
+            )
+
+        order = [(j, g) for j in range(L_TILES) for g in range(len(EXPERT_GROUPS))]
         for i, (j, g) in enumerate(order):
             experts(j, g, expert_banks[i % len(expert_banks)])
 
         for j in range(L_TILES - 1):
             terms = gather(j, 0, Z)
-            add_turned(j, terms, 0, 0, 3, nc.scalar.copy, sum_banks[0])
-            add_turned(j, terms, 0, 3, 6, nc.scalar.copy, sum_banks[1])
+            add_turned(j, terms, 0, 0, 3, sum_banks[0])
+            add_turned(j, terms, 0, 3, 6, sum_banks[1])
 
-        sums = [[merge_banks[2 * th + nh][:, :P] for nh in range(N // P)] for th in range(T // P)]
         grouped = []
         for i, (z0, z1) in enumerate(LAST_PIECES):
             terms = gather(L_TILES - 1, z0, z1)
-            copy = nc.vector.tensor_copy if z1 == Z else nc.scalar.copy
-            add_turned(L_TILES - 1, terms, z0, z0 // P, z1 // P, copy, sum_banks[i % 2])
-            grouped.append(turn_back(z0, z1, back_banks[i % 2]))
+            bank = last_sum_bank if z1 == Z else sum_banks[i % 2]
+            add_turned(L_TILES - 1, terms, z0, z0 // P, z1 // P, bank)
+            copy = nc.vector.tensor_copy if i == len(LAST_PIECES) - 2 else nc.scalar.copy
+            grouped.append(turn_back(z0, z1, back_banks[i % 2], copy))
         for piece, (z0, z1) in zip(grouped, LAST_PIECES):
-            merge(piece, z0, z1, sums)
+            nc.vector.quantize_mx(out=c_codes[:, z0:z1].bitcast(FP8X4), scales=c_scales[:, z0:z1], in_=piece[:])
+
+        late = [last_sum_bank[:, :P], back_banks[1][:, :P]]
+        for nh in range(2):
+            for o in range(HEADS - 1):
+                merge(late[nh], nh, 1, o, o == 0, False)
+        for nh in range(2):
+            for i, o in enumerate((2, 0, 1)):
+                merge(early_bank[:, nh * P : (nh + 1) * P], nh, 0, o, i == 0, i == 2)
+        for nh in range(2):
+            merge(late[nh], nh, 1, HEADS - 1, False, True)
+
+        out_rows = out.rearrange("(h p) t -> p h t", p=P)
+        result = keep.tile([P, 2, 2, P], F32, name="result")
+        nc.scalar.copy(result[:, 0, :, :], early_bank[:, : 2 * P].rearrange("p (h t) -> p h t", h=2))
+        nc.sync.dma_start(out=out_rows[:, :, :P], in_=result[:, 0, :, :])
+        nc.scalar.copy(result[:, 1, 0, :], late[0])
+        nc.scalar.dma_start(out=out_rows[:, 0, P:], in_=result[:, 1, 0, :])
+        nc.vector.tensor_copy(result[:, 1, 1, :], late[1])
+        nc.sync.dma_start(out=out_rows[:, 1, P:], in_=result[:, 1, 1, :])

@@ -59,8 +59,8 @@ def tile_moe_mhm_silu_kernel(
         ident = keep.tile([P, P], F32, name="ident")
 
         banks = [psum.tile([P, BANK], F32, name="bank%d" % b) for b in range(8)]
-        expert_banks, sum_banks, back_banks = banks[0:6], banks[4:6], banks[6:8]
-        last_sum_bank, early_bank = banks[0], banks[1]
+        sum_banks, back_banks = [banks[4:6], banks[0:2]], banks[6:8]
+        last_sum_bank, early_bank = banks[2], banks[3]
 
         nc.gpsimd.memset(xs[:, :Z].bitcast(I32), 0)
         nc.gpsimd.memset(xs[:, Z:].bitcast(I32), 0)
@@ -176,19 +176,19 @@ def tile_moe_mhm_silu_kernel(
                 stop=stop,
             )
 
-        order = [(j, g) for j in range(L_TILES) for g in range(len(EXPERT_GROUPS))]
-        for i, (j, g) in enumerate(order):
-            experts(j, g, expert_banks[i % len(expert_banks)])
+        for j in range(L_TILES):
+            for g in range(len(EXPERT_GROUPS)):
+                experts(j, g, banks[g % 4] if j == L_TILES - 1 else banks[g])
 
         for j in range(L_TILES - 1):
             terms = gather(j, 0, Z)
-            add_turned(j, terms, 0, 0, 3, sum_banks[0])
-            add_turned(j, terms, 0, 3, 6, sum_banks[1])
+            add_turned(j, terms, 0, 0, 3, sum_banks[j % 2][0])
+            add_turned(j, terms, 0, 3, 6, sum_banks[j % 2][1])
 
         grouped = []
         for i, (z0, z1) in enumerate(LAST_PIECES):
             terms = gather(L_TILES - 1, z0, z1)
-            bank = last_sum_bank if z1 == Z else sum_banks[i % 2]
+            bank = last_sum_bank if z1 == Z else sum_banks[1][i % 2]
             add_turned(L_TILES - 1, terms, z0, z0 // P, z1 // P, bank)
             copy = nc.vector.tensor_copy if i == len(LAST_PIECES) - 2 else nc.scalar.copy
             grouped.append(turn_back(z0, z1, back_banks[i % 2], copy))

@@ -26,6 +26,8 @@ LIST_COL = 16
 EXPERT_GROUPS = [(0, 4), (4, 8), (8, 12), (12, 15), (15, 17), (17, 18)]
 WORD_LOADS = [(0, 6), (6, 12), (12, 18)]
 LAST_PIECES = [(0, 256), (256, 384), (384, 512), (512, 640), (640, 768)]
+SUM_BANKS = [[4, 4, 4, 5, 5, 5], [0, 0, 1, 1, 2, 3], [4, 5, 0, 1, 2, 3]]
+PIECE_BANKS = [[4, 5], [0], [1], [4], [2]]
 
 
 def load_scale_rows(nc, plane, rows):
@@ -59,7 +61,7 @@ def tile_moe_mhm_silu_kernel(
         ident = keep.tile([P, P], F32, name="ident")
 
         banks = [psum.tile([P, BANK], F32, name="bank%d" % b) for b in range(8)]
-        sum_banks, back_banks = [banks[4:6], banks[0:2]], banks[6:8]
+        back_banks = banks[6:8]
         last_sum_bank, early_bank = banks[2], banks[3]
 
         nc.gpsimd.memset(xs[:, :Z].bitcast(I32), 0)
@@ -129,22 +131,24 @@ def tile_moe_mhm_silu_kernel(
                 terms.append(term)
             return terms
 
-        def add_turned(j, terms, z0, b0, b1, bank):
-            bank = bank[:, : (b1 - b0) * P].rearrange("p (b l) -> p b l", l=P)
-            for b in range(b0, b1):
-                for r in range(TOP):
-                    nc.tensor.matmul(
-                        bank[:, b - b0, :],
-                        terms[r][:, b * P - z0 : (b + 1) * P - z0],
-                        ident[:],
-                        start=(r == 0),
-                        stop=(r == TOP - 1),
-                        is_transpose=True,
-                    )
-            for b in range(b0, b1):
+        def add_turned(j, terms, z0, bank_ids):
+            places = [banks[k][:, len([m for m in bank_ids[:i] if m == k]) * P :][:, :P] for i, k in enumerate(bank_ids)]
+            steps = [(i, r) for i in range(len(places)) for r in range(TOP)]
+            if len(set(bank_ids)) == len(bank_ids):
+                steps = sorted(steps, key=lambda step: step[1])
+            for i, r in steps:
+                nc.tensor.matmul(
+                    places[i],
+                    terms[r][:, i * P : (i + 1) * P],
+                    ident[:],
+                    start=(r == 0),
+                    stop=(r == TOP - 1),
+                    is_transpose=True,
+                )
+            for i, place in enumerate(places):
                 nc.scalar.copy(
-                    c_rows[:, b, :, 32 * j : 32 * (j + 1), :],
-                    bank[:, b - b0, :].rearrange("z (q u e) -> z u q e", u=2, e=2),
+                    c_rows[:, z0 // P + i, :, 32 * j : 32 * (j + 1), :],
+                    place.rearrange("z (q u e) -> z u q e", u=2, e=2),
                 )
 
         def turn_back(z0, z1, bank, copy):
@@ -182,14 +186,12 @@ def tile_moe_mhm_silu_kernel(
 
         for j in range(L_TILES - 1):
             terms = gather(j, 0, Z)
-            add_turned(j, terms, 0, 0, 3, sum_banks[j % 2][0])
-            add_turned(j, terms, 0, 3, 6, sum_banks[j % 2][1])
+            add_turned(j, terms, 0, SUM_BANKS[j])
 
         grouped = []
         for i, (z0, z1) in enumerate(LAST_PIECES):
             terms = gather(L_TILES - 1, z0, z1)
-            bank = last_sum_bank if z1 == Z else sum_banks[1][i % 2]
-            add_turned(L_TILES - 1, terms, z0, z0 // P, z1 // P, bank)
+            add_turned(L_TILES - 1, terms, z0, PIECE_BANKS[i])
             copy = nc.vector.tensor_copy if i == len(LAST_PIECES) - 2 else nc.scalar.copy
             grouped.append(turn_back(z0, z1, back_banks[i % 2], copy))
         for piece, (z0, z1) in zip(grouped, LAST_PIECES):

@@ -25,9 +25,15 @@ BANK = 512
 LIST_COL = 16
 EXPERT_GROUPS = [(0, 4), (4, 8), (8, 12), (12, 15), (15, 17), (17, 18)]
 WORD_LOADS = [(0, 6), (6, 12), (12, 18)]
-LAST_PIECES = [(0, 256), (256, 384), (384, 512), (512, 640), (640, 768)]
-SUM_BANKS = [[4, 4, 4, 5, 5, 5], [0, 0, 1, 1, 2, 3], [4, 5, 0, 1, 2, 3]]
-PIECE_BANKS = [[4, 5], [0], [1], [4], [2]]
+PIECES = [
+    (0, 0, 768, [4, 4, 4, 5, 5, 5], []),
+    (1, 0, 768, [0, 0, 1, 1, 2, 3], []),
+    (2, 0, 512, [4, 4, 5, 5], []),
+    (3, 0, 512, [0, 1, 2, 3], [6, 7]),
+    (2, 512, 768, [4, 5], []),
+    (3, 512, 640, [6], [7]),
+    (3, 640, 768, [2], [6]),
+]
 
 
 def load_scale_rows(nc, plane, rows):
@@ -49,8 +55,8 @@ def tile_moe_mhm_silu_kernel(
 
         slot_list = keep.tile([P, S // LIST_COL], U16, name="slot_list")
         pos = [keep.tile([P, Z // LIST_COL], U16, name="pos%d" % r) for r in range(TOP)]
-        xw = keep.tile([P, Z], I32, name="xw", align_bytes=64)
-        xs = keep.tile([P, 2 * Z], U8, name="xs", align_bytes=64)
+        xw = keep.tile([P, 2 * Z], I32, name="xw", align_bytes=64)
+        xs = keep.tile([P, Z], U8, name="xs", align_bytes=64)
         ww = [keep.tile([P, E, H], U8, name="ww%d" % h, align_bytes=64) for h in range(2)]
         ws = [keep.tile([P, E, H // 2], U8, name="ws%d" % h, align_bytes=64) for h in range(2)]
         mw = keep.tile([P, HEADS, 2 * N], U8, name="mw", align_bytes=64)
@@ -64,11 +70,11 @@ def tile_moe_mhm_silu_kernel(
         back_banks = banks[6:8]
         last_sum_bank, early_bank = banks[2], banks[3]
 
-        nc.gpsimd.memset(xs[:, :Z].bitcast(I32), 0)
-        nc.gpsimd.memset(xs[:, Z:].bitcast(I32), 0)
-        for h in range(2):
-            nc.vector.memset(ws[h][:].bitcast(I32), 0)
-        nc.vector.memset(ms[:].bitcast(I32), 0)
+        nc.gpsimd.memset(xs[:].bitcast(I32), 0)
+        nc.vector.memset(xw[:, Z:], 0)
+        nc.vector.memset(ws[0][:].bitcast(I32), 0)
+        nc.gpsimd.memset(ws[1][:].bitcast(I32), 0)
+        nc.gpsimd.memset(ms[:].bitcast(I32), 0)
         make_identity(nc, ident[:])
 
         w_words_pe = w_words.rearrange("e s p c -> p (e s) c")
@@ -83,29 +89,29 @@ def tile_moe_mhm_silu_kernel(
                     in_=w_words_pe[:, e0:e1, h * H : (h + 1) * H].bitcast(I32),
                 )
 
-        nc.sync.dma_start(slot_list[:], offs)
-        load_scale_rows(nc, xs[:, :Z].rearrange("p (o t) -> p o t", o=HEADS), x_scales)
-        for r, pos_r in enumerate((pos1, pos2, pos3)):
-            nc.sync.dma_start(pos[r][:], pos_r)
         nc.sync.dma_start(
-            out=xw[:].rearrange("p (o t) -> p o t", o=HEADS),
+            out=xw[:, :Z].rearrange("p (o t) -> p o t", o=HEADS),
             in_=x_words.rearrange("o p t d -> p o (t d)").bitcast(I32),
         )
+        nc.sync.dma_start(slot_list[:], offs)
+        load_scale_rows(nc, xs[:].rearrange("p (o t) -> p o t", o=HEADS), x_scales)
         load_w_half(0)
+        for r, pos_r in enumerate((pos1, pos2, pos3)):
+            nc.sync.dma_start(pos[r][:], pos_r)
         for r in range(TOP):
             nc.sync.dma_start(out=gates[r][:], in_=gate[r])
         load_w_half(1)
         nc.sync.dma_start(out=mw[:].bitcast(I32), in_=wm_words.rearrange("o p c -> p o c").bitcast(I32))
         load_scale_rows(nc, ms[:], wm_scales)
 
-        slot_scales = keep.tile([P, S], U8, name="slot_scales", align_bytes=64)
+        slot_words = keep.tile([P, S], U32, name="slot_words", align_bytes=64)
         for s0 in range(0, S, S // 2):
             offsets = slot_list[:, s0 // LIST_COL : (s0 + S // 2) // LIST_COL]
-            nc.vector.tensor_copy(slot_scales[:, s0 : s0 + S // 2], xs[:].indirect(offsets))
-        slot_words = keep.tile([P, S], U32, name="slot_words", align_bytes=64)
+            nc.vector.tensor_copy(slot_words[:, s0 : s0 + S // 2], xw[:].bitcast(U32).indirect(offsets))
+        slot_scales = keep.tile([P, S], U8, name="slot_scales", align_bytes=64)
         for e0, e1 in EXPERT_GROUPS:
             offsets = slot_list[:, e0 * C // LIST_COL : e1 * C // LIST_COL]
-            nc.vector.tensor_copy(slot_words[:, e0 * C : e1 * C], xw[:].bitcast(U32).indirect(offsets))
+            nc.vector.tensor_copy(slot_scales[:, e0 * C : e1 * C], xs[:].indirect(offsets))
 
         def experts(j, g, bank):
             e0, e1 = EXPERT_GROUPS[g]
@@ -151,18 +157,17 @@ def tile_moe_mhm_silu_kernel(
                     place.rearrange("z (q u e) -> z u q e", u=2, e=2),
                 )
 
-        def turn_back(z0, z1, bank, copy):
-            blocks = (z1 - z0) // P
-            bank = bank[:, : blocks * 2 * P].rearrange("p (b u z) -> p b u z", u=2, z=P)
-            for b in range(blocks):
-                for u in range(2):
-                    pairs = c_rows[:, z0 // P + b, u, :, :].rearrange("z p e -> z (p e)").bitcast(F32)
-                    nc.tensor.transpose(bank[:, b, u, :], pairs, ident[:])
+        def turn_back(z0, z1, bank_ids, copy):
             grouped = keep.tile([P, 4 * (z1 - z0)], BF16, name="grouped%d" % z0, align_bytes=64)
-            copy(
-                grouped[:].bitcast(F32).rearrange("p (b z u) -> p b z u", b=blocks, u=2),
-                bank.rearrange("p b u z -> p b z u"),
-            )
+            blocks = (z1 - z0) // P // len(bank_ids)
+            for i, k in enumerate(bank_ids):
+                bank = banks[k][:, : blocks * 2 * P].rearrange("p (b u z) -> p b u z", u=2, z=P)
+                for b in range(blocks):
+                    for u in range(2):
+                        pairs = c_rows[:, z0 // P + i * blocks + b, u, :, :].rearrange("z p e -> z (p e)").bitcast(F32)
+                        nc.tensor.transpose(bank[:, b, u, :], pairs, ident[:])
+                words = grouped[:].bitcast(F32)[:, i * blocks * 2 * P : (i + 1) * blocks * 2 * P]
+                copy(words.rearrange("p (b z u) -> p b z u", b=blocks, u=2), bank.rearrange("p b u z -> p b z u"))
             return grouped
 
         c_codes = keep.tile([P, Z], U32, name="c_codes", align_bytes=64)
@@ -184,17 +189,14 @@ def tile_moe_mhm_silu_kernel(
             for g in range(len(EXPERT_GROUPS)):
                 experts(j, g, banks[g % 4] if j == L_TILES - 1 else banks[g])
 
-        for j in range(L_TILES - 1):
-            terms = gather(j, 0, Z)
-            add_turned(j, terms, 0, SUM_BANKS[j])
-
         grouped = []
-        for i, (z0, z1) in enumerate(LAST_PIECES):
-            terms = gather(L_TILES - 1, z0, z1)
-            add_turned(L_TILES - 1, terms, z0, PIECE_BANKS[i])
-            copy = nc.vector.tensor_copy if i == len(LAST_PIECES) - 2 else nc.scalar.copy
-            grouped.append(turn_back(z0, z1, back_banks[i % 2], copy))
-        for piece, (z0, z1) in zip(grouped, LAST_PIECES):
+        for i, (j, z0, z1, sum_banks, turn_banks) in enumerate(PIECES):
+            terms = gather(j, z0, z1)
+            add_turned(j, terms, z0, sum_banks)
+            copy = nc.vector.tensor_copy if i == len(PIECES) - 2 else nc.scalar.copy
+            if turn_banks:
+                grouped.append((turn_back(z0, z1, turn_banks, copy), z0, z1))
+        for piece, z0, z1 in grouped:
             nc.vector.quantize_mx(out=c_codes[:, z0:z1].bitcast(FP8X4), scales=c_scales[:, z0:z1], in_=piece[:])
 
         late = [last_sum_bank[:, :P], back_banks[1][:, :P]]

@@ -26,11 +26,12 @@ LIST_COL = 16
 EXPERT_GROUPS = [(0, 4), (4, 8), (8, 12), (12, 15), (15, 17), (17, 18)]
 WORD_LOADS = [(0, 6), (6, 12), (12, 18)]
 PIECES = [
-    (0, 0, 768, [4, 4, 4, 5, 5, 5], []),
-    (1, 0, 768, [0, 0, 1, 1, 2, 3], []),
-    (2, 0, 512, [4, 4, 5, 5], []),
+    (0, 0, 768, [0, 0, 0, 0, 3, 3], []),
+    (1, 0, 512, [1, 1, 1, 1], []),
+    (2, 0, 512, [4, 4, 4, 4], []),
     (3, 0, 512, [0, 1, 2, 3], [6, 7]),
-    (2, 512, 768, [4, 5], []),
+    (1, 512, 768, [4, 5], []),
+    (2, 512, 768, [0, 1], []),
     (3, 512, 640, [6], [7]),
     (3, 640, 768, [2], [6]),
 ]
@@ -55,14 +56,14 @@ def tile_moe_mhm_silu_kernel(
 
         slot_list = keep.tile([P, S // LIST_COL], U16, name="slot_list")
         pos = [keep.tile([P, Z // LIST_COL], U16, name="pos%d" % r) for r in range(TOP)]
-        xw = keep.tile([P, 2 * Z], I32, name="xw", align_bytes=64)
-        xs = keep.tile([P, Z], U8, name="xs", align_bytes=64)
+        xw = keep.tile([P, Z], I32, name="xw", align_bytes=64)
+        xs = keep.tile([P, 2 * Z], U8, name="xs", align_bytes=64)
         ww = [keep.tile([P, E, H], U8, name="ww%d" % h, align_bytes=64) for h in range(2)]
         ws = [keep.tile([P, E, H // 2], U8, name="ws%d" % h, align_bytes=64) for h in range(2)]
         mw = keep.tile([P, HEADS, 2 * N], U8, name="mw", align_bytes=64)
         ms = keep.tile([P, HEADS, N], U8, name="ms", align_bytes=64)
         gates = [keep.tile([P, Z], F32, name="gate%d" % r) for r in range(TOP)]
-        y = [keep.tile([P, S], F32, name="y%d" % j) for j in range(L_TILES)]
+        y = [keep.tile([P, S], F32, name="y%d" % j, tag="y%d" % j, align_bytes=64) for j in range(L_TILES)]
         c_rows = keep.tile([P, Z // P, 2, P, 2], BF16, name="c_rows", align_bytes=64)
         ident = keep.tile([P, P], F32, name="ident")
 
@@ -70,10 +71,10 @@ def tile_moe_mhm_silu_kernel(
         back_banks = banks[6:8]
         last_sum_bank, early_bank = banks[2], banks[3]
 
-        nc.gpsimd.memset(xs[:].bitcast(I32), 0)
-        nc.vector.memset(xw[:, Z:], 0)
-        nc.vector.memset(ws[0][:].bitcast(I32), 0)
-        nc.gpsimd.memset(ws[1][:].bitcast(I32), 0)
+        nc.gpsimd.memset(xs[:, :Z].bitcast(I32), 0)
+        nc.gpsimd.memset(xs[:, Z:].bitcast(I32), 0)
+        for h in range(2):
+            nc.vector.memset(ws[h][:].bitcast(I32), 0)
         nc.gpsimd.memset(ms[:].bitcast(I32), 0)
         make_identity(nc, ident[:])
 
@@ -89,32 +90,31 @@ def tile_moe_mhm_silu_kernel(
                     in_=w_words_pe[:, e0:e1, h * H : (h + 1) * H].bitcast(I32),
                 )
 
-        nc.sync.dma_start(
-            out=xw[:, :Z].rearrange("p (o t) -> p o t", o=HEADS),
-            in_=x_words.rearrange("o p t d -> p o (t d)").bitcast(I32),
-        )
         nc.sync.dma_start(slot_list[:], offs)
-        load_scale_rows(nc, xs[:].rearrange("p (o t) -> p o t", o=HEADS), x_scales)
-        load_w_half(0)
+        load_scale_rows(nc, xs[:, :Z].rearrange("p (o t) -> p o t", o=HEADS), x_scales)
         for r, pos_r in enumerate((pos1, pos2, pos3)):
             nc.sync.dma_start(pos[r][:], pos_r)
+        nc.sync.dma_start(
+            out=xw[:].rearrange("p (o t) -> p o t", o=HEADS),
+            in_=x_words.rearrange("o p t d -> p o (t d)").bitcast(I32),
+        )
+        load_w_half(0)
         for r in range(TOP):
             nc.sync.dma_start(out=gates[r][:], in_=gate[r])
         load_w_half(1)
         nc.sync.dma_start(out=mw[:].bitcast(I32), in_=wm_words.rearrange("o p c -> p o c").bitcast(I32))
         load_scale_rows(nc, ms[:], wm_scales)
 
-        slot_words = keep.tile([P, S], U32, name="slot_words", align_bytes=64)
+        slot_scales = keep.tile([P, S], U8, name="slot_scales", align_bytes=64)
         for s0 in range(0, S, S // 2):
             offsets = slot_list[:, s0 // LIST_COL : (s0 + S // 2) // LIST_COL]
-            nc.vector.tensor_copy(slot_words[:, s0 : s0 + S // 2], xw[:].bitcast(U32).indirect(offsets))
-        slot_scales = keep.tile([P, S], U8, name="slot_scales", align_bytes=64)
+            nc.vector.tensor_copy(slot_scales[:, s0 : s0 + S // 2], xs[:].indirect(offsets))
+        slot_words = keep.tile([P, S], U32, name="slot_words", align_bytes=64)
         for e0, e1 in EXPERT_GROUPS:
             offsets = slot_list[:, e0 * C // LIST_COL : e1 * C // LIST_COL]
-            nc.vector.tensor_copy(slot_scales[:, e0 * C : e1 * C], xs[:].indirect(offsets))
+            nc.vector.tensor_copy(slot_words[:, e0 * C : e1 * C], xw[:].bitcast(U32).indirect(offsets))
 
-        def experts(j, g, bank):
-            e0, e1 = EXPERT_GROUPS[g]
+        def experts(j, e0, e1, bank):
             for e in range(e0, e1):
                 cols = slice((e - e0) * C, (e - e0 + 1) * C)
                 nc.tensor.matmul_mx(
@@ -151,10 +151,11 @@ def tile_moe_mhm_silu_kernel(
                     stop=(r == TOP - 1),
                     is_transpose=True,
                 )
-            for i, place in enumerate(places):
+            for k in sorted(set(bank_ids), key=bank_ids.index):
+                first, count = z0 // P + bank_ids.index(k), bank_ids.count(k)
                 nc.scalar.copy(
-                    c_rows[:, z0 // P + i, :, 32 * j : 32 * (j + 1), :],
-                    place.rearrange("z (q u e) -> z u q e", u=2, e=2),
+                    c_rows[:, first : first + count, :, 32 * j : 32 * (j + 1), :],
+                    banks[k][:, : count * P].rearrange("z (b q u e) -> z b u q e", b=count, u=2, e=2),
                 )
 
         def turn_back(z0, z1, bank_ids, copy):
@@ -170,7 +171,6 @@ def tile_moe_mhm_silu_kernel(
                 copy(words.rearrange("p (b z u) -> p b z u", b=blocks, u=2), bank.rearrange("p b u z -> p b z u"))
             return grouped
 
-        c_codes = keep.tile([P, Z], U32, name="c_codes", align_bytes=64)
         c_scales = keep.tile([P, Z], U8, name="c_scales", align_bytes=64)
 
         def merge(sums, nh, th, o, start, stop):
@@ -185,9 +185,11 @@ def tile_moe_mhm_silu_kernel(
                 stop=stop,
             )
 
-        for j in range(L_TILES):
-            for g in range(len(EXPERT_GROUPS)):
-                experts(j, g, banks[g % 4] if j == L_TILES - 1 else banks[g])
+        for g, (e0, e1) in enumerate(EXPERT_GROUPS):
+            experts(0, e0, e1, banks[g])
+        for j in range(1, L_TILES):
+            for g, e0 in enumerate(range(0, E, 4)):
+                experts(j, e0, min(e0 + 4, E), banks[g % 4] if j == L_TILES - 1 else banks[g])
 
         grouped = []
         for i, (j, z0, z1, sum_banks, turn_banks) in enumerate(PIECES):
@@ -196,6 +198,7 @@ def tile_moe_mhm_silu_kernel(
             copy = nc.vector.tensor_copy if i == len(PIECES) - 2 else nc.scalar.copy
             if turn_banks:
                 grouped.append((turn_back(z0, z1, turn_banks, copy), z0, z1))
+        c_codes = keep.tile([P, Z], U32, name="c_codes", tag="y%d" % (L_TILES - 1), align_bytes=64)
         for piece, z0, z1 in grouped:
             nc.vector.quantize_mx(out=c_codes[:, z0:z1].bitcast(FP8X4), scales=c_scales[:, z0:z1], in_=piece[:])
 

@@ -27,19 +27,18 @@ EXPERT_GROUPS = [(0, 4), (4, 8), (8, 12), (12, 15), (15, 17), (17, 18)]
 WORD_LOADS = [(0, 6), (6, 12), (12, 18)]
 PIECES = [
     (0, 0, 768, [0, 0, 0, 0, 3, 3], []),
-    (1, 0, 512, [1, 1, 1, 1], []),
+    (1, 0, 768, [1, 1, 1, 1, 2, 2], []),
     (2, 0, 512, [4, 4, 4, 4], []),
     (3, 0, 512, [0, 1, 2, 3], [6, 7]),
-    (1, 512, 768, [4, 5], []),
-    (2, 512, 768, [0, 1], []),
+    (2, 512, 768, [4, 5], []),
     (3, 512, 640, [6], [7]),
     (3, 640, 768, [2], [6]),
 ]
 
 
-def load_scale_rows(nc, plane, rows):
+def load_scale_rows(queues, plane, rows):
     for q in range(4):
-        nc.sync.dma_start(
+        queues[q % len(queues)].dma_start(
             out=plane[32 * q : 32 * q + 4].bitcast(I32),
             in_=rows[:, 4 * q : 4 * q + 4, :].rearrange("a b n -> b a n").bitcast(I32),
         )
@@ -51,7 +50,7 @@ def tile_moe_mhm_silu_kernel(
     nc = tc.nc
     with ExitStack() as ctx:
         keep = ctx.enter_context(tc.tile_pool(name="keep", bufs=1))
-        ring = ctx.enter_context(tc.tile_pool(name="ring", bufs=3))
+        ring = ctx.enter_context(tc.tile_pool(name="ring", bufs=7))
         psum = ctx.enter_context(tc.psum_pool(name="psum", bufs=1))
 
         slot_list = keep.tile([P, S // LIST_COL], U16, name="slot_list")
@@ -73,8 +72,8 @@ def tile_moe_mhm_silu_kernel(
 
         nc.gpsimd.memset(xs[:, :Z].bitcast(I32), 0)
         nc.gpsimd.memset(xs[:, Z:].bitcast(I32), 0)
-        for h in range(2):
-            nc.vector.memset(ws[h][:].bitcast(I32), 0)
+        nc.vector.memset(ws[0][:].bitcast(I32), 0)
+        nc.gpsimd.memset(ws[1][:].bitcast(I32), 0)
         nc.gpsimd.memset(ms[:].bitcast(I32), 0)
         make_identity(nc, ident[:])
 
@@ -83,7 +82,7 @@ def tile_moe_mhm_silu_kernel(
         w_scales_eb = w_scales.rearrange("e s b l -> (e s) b l")
 
         def load_w_half(h):
-            load_scale_rows(nc, ws[h][:], w_scales_eb[:, :, h * H // 2 : (h + 1) * H // 2])
+            load_scale_rows([nc.sync], ws[h][:], w_scales_eb[:, :, h * H // 2 : (h + 1) * H // 2])
             for e0, e1 in WORD_LOADS:
                 nc.sync.dma_start(
                     out=ww[h][:, e0:e1, :].bitcast(I32),
@@ -91,7 +90,7 @@ def tile_moe_mhm_silu_kernel(
                 )
 
         nc.sync.dma_start(slot_list[:], offs)
-        load_scale_rows(nc, xs[:, :Z].rearrange("p (o t) -> p o t", o=HEADS), x_scales)
+        load_scale_rows([nc.scalar, nc.sync], xs[:, :Z].rearrange("p (o t) -> p o t", o=HEADS), x_scales)
         for r, pos_r in enumerate((pos1, pos2, pos3)):
             nc.sync.dma_start(pos[r][:], pos_r)
         nc.sync.dma_start(
@@ -103,7 +102,7 @@ def tile_moe_mhm_silu_kernel(
             nc.sync.dma_start(out=gates[r][:], in_=gate[r])
         load_w_half(1)
         nc.sync.dma_start(out=mw[:].bitcast(I32), in_=wm_words.rearrange("o p c -> p o c").bitcast(I32))
-        load_scale_rows(nc, ms[:], wm_scales)
+        load_scale_rows([nc.sync], ms[:], wm_scales)
 
         slot_scales = keep.tile([P, S], U8, name="slot_scales", align_bytes=64)
         for s0 in range(0, S, S // 2):

@@ -30,17 +30,17 @@ PIECES = [
     (1, 0, 768, [1, 1, 1, 1, 2, 2], []),
     (2, 0, 512, [4, 4, 4, 4], []),
     (3, 0, 512, [0, 1, 2, 3], [6, 7]),
-    (2, 512, 768, [4, 5], []),
-    (3, 512, 640, [6], [7]),
-    (3, 640, 768, [2], [6]),
+    (2, 512, 768, [4, 4], []),
+    (3, 512, 640, [2], [5]),
+    (3, 640, 768, [3], [6]),
 ]
 
 
 def load_scale_rows(queues, plane, rows):
-    for q in range(4):
-        queues[q % len(queues)].dma_start(
-            out=plane[32 * q : 32 * q + 4].bitcast(I32),
-            in_=rows[:, 4 * q : 4 * q + 4, :].rearrange("a b n -> b a n").bitcast(I32),
+    for b in range(4):
+        queues[b % len(queues)].dma_start(
+            out=plane[b:P:32].bitcast(I32),
+            in_=rows[:, b:16:4, :].rearrange("a q n -> q a n").bitcast(I32),
         )
 
 
@@ -67,8 +67,7 @@ def tile_moe_mhm_silu_kernel(
         ident = keep.tile([P, P], F32, name="ident")
 
         banks = [psum.tile([P, BANK], F32, name="bank%d" % b) for b in range(8)]
-        back_banks = banks[6:8]
-        last_sum_bank, early_bank = banks[2], banks[3]
+        last_sum_bank, early_bank = banks[3], banks[2]
 
         nc.gpsimd.memset(xs[:, :Z].bitcast(I32), 0)
         nc.gpsimd.memset(xs[:, Z:].bitcast(I32), 0)
@@ -125,6 +124,8 @@ def tile_moe_mhm_silu_kernel(
                     start=True,
                     stop=True,
                 )
+
+        def silu(j, e0, e1, bank):
             nc.scalar.activation(y[j][:, e0 * C : e1 * C], bank[:, : (e1 - e0) * C], SILU)
 
         def gather(j, z0, z1):
@@ -138,16 +139,15 @@ def tile_moe_mhm_silu_kernel(
 
         def add_turned(j, terms, z0, bank_ids):
             places = [banks[k][:, len([m for m in bank_ids[:i] if m == k]) * P :][:, :P] for i, k in enumerate(bank_ids)]
-            steps = [(i, r) for i in range(len(places)) for r in range(TOP)]
-            if len(set(bank_ids)) == len(bank_ids):
-                steps = sorted(steps, key=lambda step: step[1])
+            steps = [(i, r) for r in range(TOP) for i in range(len(places))]
             for i, r in steps:
+                k = bank_ids[i]
                 nc.tensor.matmul(
                     places[i],
                     terms[r][:, i * P : (i + 1) * P],
                     ident[:],
-                    start=(r == 0),
-                    stop=(r == TOP - 1),
+                    start=(r == 0 and k not in bank_ids[:i]),
+                    stop=(r == TOP - 1 and k not in bank_ids[i + 1 :]),
                     is_transpose=True,
                 )
             for k in sorted(set(bank_ids), key=bank_ids.index):
@@ -186,9 +186,17 @@ def tile_moe_mhm_silu_kernel(
 
         for g, (e0, e1) in enumerate(EXPERT_GROUPS):
             experts(0, e0, e1, banks[g])
+            silu(0, e0, e1, banks[g])
+            if g < 2:
+                experts(1, e0, e1, banks[6 + g])
         for j in range(1, L_TILES):
             for g, e0 in enumerate(range(0, E, 4)):
-                experts(j, e0, min(e0 + 4, E), banks[g % 4] if j == L_TILES - 1 else banks[g])
+                bank = banks[g % 4] if j == L_TILES - 1 else banks[g]
+                if j == 1 and g < 2:
+                    bank = banks[6 + g]
+                else:
+                    experts(j, e0, min(e0 + 4, E), bank)
+                silu(j, e0, min(e0 + 4, E), bank)
 
         grouped = []
         for i, (j, z0, z1, sum_banks, turn_banks) in enumerate(PIECES):
@@ -201,7 +209,7 @@ def tile_moe_mhm_silu_kernel(
         for piece, z0, z1 in grouped:
             nc.vector.quantize_mx(out=c_codes[:, z0:z1].bitcast(FP8X4), scales=c_scales[:, z0:z1], in_=piece[:])
 
-        late = [last_sum_bank[:, :P], back_banks[1][:, :P]]
+        late = [last_sum_bank[:, :P], banks[5][:, :P]]
         for nh in range(2):
             for o in range(HEADS - 1):
                 merge(late[nh], nh, 1, o, o == 0, False)

@@ -31,8 +31,7 @@ PIECES = [
     (2, 0, 512, [4, 4, 4, 4], []),
     (3, 0, 512, [0, 1, 2, 3], [6, 7]),
     (2, 512, 768, [4, 4], []),
-    (3, 512, 640, [2], [5]),
-    (3, 640, 768, [3], [6]),
+    (3, 512, 768, [2, 3], [5, 6]),
 ]
 
 
@@ -67,7 +66,6 @@ def tile_moe_mhm_silu_kernel(
         ident = keep.tile([P, P], F32, name="ident")
 
         banks = [psum.tile([P, BANK], F32, name="bank%d" % b) for b in range(8)]
-        last_sum_bank, early_bank = banks[3], banks[2]
 
         nc.gpsimd.memset(xs[:, :Z].bitcast(I32), 0)
         nc.gpsimd.memset(xs[:, Z:].bitcast(I32), 0)
@@ -128,12 +126,16 @@ def tile_moe_mhm_silu_kernel(
         def silu(j, e0, e1, bank):
             nc.scalar.activation(y[j][:, e0 * C : e1 * C], bank[:, : (e1 - e0) * C], SILU)
 
-        def gather(j, z0, z1):
+        def gather(j, z0, z1, by_block):
             terms = []
             for r in range(TOP):
                 term = ring.tile([P, z1 - z0], F32, name="term", tag="term%d" % r)
-                offsets = pos[r][:, z0 // LIST_COL : z1 // LIST_COL]
-                nc.vector.tensor_tensor(term[:], y[j][:].indirect(offsets), gates[r][:, z0:z1], MULT)
+                step = P if (by_block and r == TOP - 1) else z1 - z0
+                for a in range(z0, z1, step):
+                    offsets = pos[r][:, a // LIST_COL : (a + step) // LIST_COL]
+                    nc.vector.tensor_tensor(
+                        term[:, a - z0 : a - z0 + step], y[j][:].indirect(offsets), gates[r][:, a : a + step], MULT
+                    )
                 terms.append(term)
             return terms
 
@@ -200,30 +202,32 @@ def tile_moe_mhm_silu_kernel(
 
         grouped = []
         for i, (j, z0, z1, sum_banks, turn_banks) in enumerate(PIECES):
-            terms = gather(j, z0, z1)
+            last = i == len(PIECES) - 1
+            terms = gather(j, z0, z1, last)
             add_turned(j, terms, z0, sum_banks)
-            copy = nc.vector.tensor_copy if i == len(PIECES) - 2 else nc.scalar.copy
-            if turn_banks:
-                grouped.append((turn_back(z0, z1, turn_banks, copy), z0, z1))
+            if last:
+                grouped.append((turn_back(z0, z0 + P, turn_banks[:1], nc.vector.tensor_copy), z0, z0 + P))
+                grouped.append((turn_back(z0 + P, z1, turn_banks[1:], nc.scalar.copy), z0 + P, z1))
+            elif turn_banks:
+                grouped.append((turn_back(z0, z1, turn_banks, nc.scalar.copy), z0, z1))
         c_codes = keep.tile([P, Z], U32, name="c_codes", tag="y%d" % (L_TILES - 1), align_bytes=64)
         for piece, z0, z1 in grouped:
             nc.vector.quantize_mx(out=c_codes[:, z0:z1].bitcast(FP8X4), scales=c_scales[:, z0:z1], in_=piece[:])
 
-        late = [last_sum_bank[:, :P], banks[5][:, :P]]
+        late = [banks[3][:, :P], banks[5][:, :P]]
+        early = [banks[0][:, :P], banks[1][:, :P]]
         for nh in range(2):
             for o in range(HEADS - 1):
                 merge(late[nh], nh, 1, o, o == 0, False)
         for nh in range(2):
             for i, o in enumerate((2, 0, 1)):
-                merge(early_bank[:, nh * P : (nh + 1) * P], nh, 0, o, i == 0, i == 2)
+                merge(early[nh], nh, 0, o, i == 0, i == 2)
         for nh in range(2):
             merge(late[nh], nh, 1, HEADS - 1, False, True)
 
-        out_rows = out.rearrange("(h p) t -> p h t", p=P)
         result = keep.tile([P, 2, 2, P], F32, name="result")
-        nc.scalar.copy(result[:, 0, :, :], early_bank[:, : 2 * P].rearrange("p (h t) -> p h t", h=2))
-        nc.sync.dma_start(out=out_rows[:, :, :P], in_=result[:, 0, :, :])
-        nc.scalar.copy(result[:, 1, 0, :], late[0])
-        nc.scalar.dma_start(out=out_rows[:, 0, P:], in_=result[:, 1, 0, :])
-        nc.vector.tensor_copy(result[:, 1, 1, :], late[1])
-        nc.sync.dma_start(out=out_rows[:, 1, P:], in_=result[:, 1, 1, :])
+        for th, sums in enumerate((early, late)):
+            nc.scalar.copy(result[:, th, 0, :], sums[0])
+            nc.scalar.dma_start(out=out[:P, th * P : (th + 1) * P], in_=result[:, th, 0, :])
+            nc.vector.tensor_copy(result[:, th, 1, :], sums[1])
+            nc.sync.dma_start(out=out[P:, th * P : (th + 1) * P], in_=result[:, th, 1, :])

@@ -25,14 +25,6 @@ BANK = 512
 LIST_COL = 16
 EXPERT_GROUPS = [(0, 4), (4, 8), (8, 12), (12, 15), (15, 17), (17, 18)]
 WORD_LOADS = [(0, 6), (6, 12), (12, 18)]
-PIECES = [
-    (0, 0, 768, [0, 0, 0, 0, 3, 3], []),
-    (1, 0, 768, [1, 1, 1, 1, 2, 2], []),
-    (2, 0, 512, [4, 4, 4, 4], []),
-    (3, 0, 512, [0, 1, 2, 3], [6, 7]),
-    (2, 512, 768, [4, 4], []),
-    (3, 512, 768, [2, 3], [5, 6]),
-]
 
 
 def load_scale_rows(queues, plane, rows):
@@ -49,7 +41,7 @@ def tile_moe_mhm_silu_kernel(
     nc = tc.nc
     with ExitStack() as ctx:
         keep = ctx.enter_context(tc.tile_pool(name="keep", bufs=1))
-        ring = ctx.enter_context(tc.tile_pool(name="ring", bufs=7))
+        ring = ctx.enter_context(tc.tile_pool(name="ring", bufs=4))
         psum = ctx.enter_context(tc.psum_pool(name="psum", bufs=1))
 
         slot_list = keep.tile([P, S // LIST_COL], U16, name="slot_list")
@@ -62,7 +54,7 @@ def tile_moe_mhm_silu_kernel(
         ms = keep.tile([P, HEADS, N], U8, name="ms", align_bytes=64)
         gates = [keep.tile([P, Z], F32, name="gate%d" % r) for r in range(TOP)]
         y = [keep.tile([P, S], F32, name="y%d" % j, tag="y%d" % j, align_bytes=64) for j in range(L_TILES)]
-        c_rows = keep.tile([P, Z // P, 2, P, 2], BF16, name="c_rows", align_bytes=64)
+        c_rows = keep.tile([P, HEADS, 2, 2, P, 2], BF16, name="c_rows", align_bytes=64)
         ident = keep.tile([P, P], F32, name="ident")
 
         banks = [psum.tile([P, BANK], F32, name="bank%d" % b) for b in range(8)]
@@ -98,8 +90,17 @@ def tile_moe_mhm_silu_kernel(
         for r in range(TOP):
             nc.sync.dma_start(out=gates[r][:], in_=gate[r])
         load_w_half(1)
-        nc.sync.dma_start(out=mw[:].bitcast(I32), in_=wm_words.rearrange("o p c -> p o c").bitcast(I32))
-        load_scale_rows([nc.sync], ms[:], wm_scales)
+        for o in range(HEADS):
+            nc.sync.dma_start(
+                out=mw[32 * o : 32 * (o + 1)].bitcast(I32),
+                in_=wm_words[o, 32:, :].rearrange("(a p) c -> p a c", p=32).bitcast(I32),
+            )
+            nc.sync.dma_start(
+                out=ms[32 * o : 32 * o + 4].bitcast(I32),
+                in_=wm_scales[o, 4:, :].rearrange("(a b) n -> b a n", b=4).bitcast(I32),
+            )
+        nc.sync.dma_start(out=mw[96:].bitcast(I32), in_=wm_words[:, :32, :].rearrange("a p c -> p a c").bitcast(I32))
+        nc.sync.dma_start(out=ms[96:100].bitcast(I32), in_=wm_scales[:, :4, :].rearrange("a b n -> b a n").bitcast(I32))
 
         slot_scales = keep.tile([P, S], U8, name="slot_scales", align_bytes=64)
         for s0 in range(0, S, S // 2):
@@ -126,51 +127,44 @@ def tile_moe_mhm_silu_kernel(
         def silu(j, e0, e1, bank):
             nc.scalar.activation(y[j][:, e0 * C : e1 * C], bank[:, : (e1 - e0) * C], SILU)
 
-        def gather(j, z0, z1, by_block):
-            terms = []
+        def gather(j, r, pieces):
+            term = ring.tile([P, Z], F32, name="term", tag="term%d" % r)
+            for b0, b1 in pieces:
+                z0, z1 = b0 * P, b1 * P
+                offsets = pos[r][:, z0 // LIST_COL : z1 // LIST_COL]
+                nc.vector.tensor_tensor(term[:, z0:z1], y[j][:].indirect(offsets), gates[r][:, z0:z1], MULT)
+            return term
+
+        def add_turned(terms, groups, order):
             for r in range(TOP):
-                term = ring.tile([P, z1 - z0], F32, name="term", tag="term%d" % r)
-                step = P if (by_block and r == TOP - 1) else z1 - z0
-                for a in range(z0, z1, step):
-                    offsets = pos[r][:, a // LIST_COL : (a + step) // LIST_COL]
-                    nc.vector.tensor_tensor(
-                        term[:, a - z0 : a - z0 + step], y[j][:].indirect(offsets), gates[r][:, a : a + step], MULT
+                for b in order:
+                    k, blocks = [group for group in groups if b in group[1]][0]
+                    i = blocks.index(b)
+                    nc.tensor.matmul(
+                        banks[k][:, i * P : (i + 1) * P],
+                        terms[r][:, b * P : (b + 1) * P],
+                        ident[:],
+                        start=(r == 0 and i == 0),
+                        stop=(r == TOP - 1 and i == len(blocks) - 1),
+                        is_transpose=True,
                     )
-                terms.append(term)
-            return terms
 
-        def add_turned(j, terms, z0, bank_ids):
-            places = [banks[k][:, len([m for m in bank_ids[:i] if m == k]) * P :][:, :P] for i, k in enumerate(bank_ids)]
-            steps = [(i, r) for r in range(TOP) for i in range(len(places))]
-            for i, r in steps:
-                k = bank_ids[i]
-                nc.tensor.matmul(
-                    places[i],
-                    terms[r][:, i * P : (i + 1) * P],
-                    ident[:],
-                    start=(r == 0 and k not in bank_ids[:i]),
-                    stop=(r == TOP - 1 and k not in bank_ids[i + 1 :]),
-                    is_transpose=True,
-                )
-            for k in sorted(set(bank_ids), key=bank_ids.index):
-                first, count = z0 // P + bank_ids.index(k), bank_ids.count(k)
-                nc.scalar.copy(
-                    c_rows[:, first : first + count, :, 32 * j : 32 * (j + 1), :],
-                    banks[k][:, : count * P].rearrange("z (b q u e) -> z b u q e", b=count, u=2, e=2),
-                )
+        def round_rows(j, k, blocks):
+            th, heads = blocks[0] % 2, slice(blocks[0] // 2, blocks[-1] // 2 + 1)
+            sums = banks[k][:, : len(blocks) * P].rearrange("z (o q u e) -> z o u q e", u=2, e=2, q=32)
+            if j == 0:
+                rows = c_rows[:, heads, th, :, 96:, :]
+            else:
+                rows = c_rows[:, j - 1, th].rearrange("z u (o q) e -> z o u q e", q=32)[:, heads]
+            nc.scalar.copy(rows, sums)
 
-        def turn_back(z0, z1, bank_ids, copy):
-            grouped = keep.tile([P, 4 * (z1 - z0)], BF16, name="grouped%d" % z0, align_bytes=64)
-            blocks = (z1 - z0) // P // len(bank_ids)
-            for i, k in enumerate(bank_ids):
-                bank = banks[k][:, : blocks * 2 * P].rearrange("p (b u z) -> p b u z", u=2, z=P)
-                for b in range(blocks):
-                    for u in range(2):
-                        pairs = c_rows[:, z0 // P + i * blocks + b, u, :, :].rearrange("z p e -> z (p e)").bitcast(F32)
-                        nc.tensor.transpose(bank[:, b, u, :], pairs, ident[:])
-                words = grouped[:].bitcast(F32)[:, i * blocks * 2 * P : (i + 1) * blocks * 2 * P]
-                copy(words.rearrange("p (b z u) -> p b z u", b=blocks, u=2), bank.rearrange("p b u z -> p b z u"))
-            return grouped
+        def turn_back(a, halves, k, words, copy):
+            bank = banks[k][:, : len(halves) * 2 * P].rearrange("p (b u z) -> p b u z", u=2, z=P)
+            for i, th in enumerate(halves):
+                for u in range(2):
+                    pairs = c_rows[:, a, th, u, :, :].rearrange("z p e -> z (p e)").bitcast(F32)
+                    nc.tensor.transpose(bank[:, i, u, :], pairs, ident[:])
+            copy(words.rearrange("p (b z u) -> p b z u", z=P, u=2), bank.rearrange("p b u z -> p b z u"))
 
         c_scales = keep.tile([P, Z], U8, name="c_scales", align_bytes=64)
 
@@ -200,22 +194,30 @@ def tile_moe_mhm_silu_kernel(
                     experts(j, e0, min(e0 + 4, E), bank)
                 silu(j, e0, min(e0 + 4, E), bank)
 
-        grouped = []
-        for i, (j, z0, z1, sum_banks, turn_banks) in enumerate(PIECES):
-            last = i == len(PIECES) - 1
-            terms = gather(j, z0, z1, last)
-            add_turned(j, terms, z0, sum_banks)
-            if last:
-                grouped.append((turn_back(z0, z0 + P, turn_banks[:1], nc.vector.tensor_copy), z0, z0 + P))
-                grouped.append((turn_back(z0 + P, z1, turn_banks[1:], nc.scalar.copy), z0 + P, z1))
-            elif turn_banks:
-                grouped.append((turn_back(z0, z1, turn_banks, nc.scalar.copy), z0, z1))
+        early_c = keep.tile([P, 4 * 2 * T], BF16, name="early_c", align_bytes=64)
+        last_c = [keep.tile([P, 4 * P], BF16, name="last_c%d" % th, align_bytes=64) for th in range(2)]
+        for j, (k0, k1) in enumerate([(0, 3), (1, 2), (4, 5)]):
+            groups = [(k0, [0, 2, 4]), (k1, [1, 3, 5])]
+            add_turned([gather(j, r, [(0, 6)]) for r in range(TOP)], groups, [0, 2, 4, 1, 3, 5])
+            for group in groups:
+                round_rows(j, *group)
+            if j > 0:
+                words = early_c[:].bitcast(F32)[:, (j - 1) * 2 * T : j * 2 * T]
+                turn_back(j - 1, [0, 1], 5 + j, words, nc.scalar.copy)
+        j = L_TILES - 1
+        groups = [(0, [0, 2, 4]), (1, [1, 3]), (3, [5])]
+        terms = [gather(j, 0, [(0, 6)]), gather(j, 1, [(0, 6)]), gather(j, 2, [(0, 3), (4, 5), (3, 4), (5, 6)])]
+        add_turned(terms, groups, [0, 2, 1, 4, 3, 5])
+        for group in groups:
+            round_rows(j, *group)
+        turn_back(2, [0], 4, last_c[0][:].bitcast(F32), nc.vector.tensor_copy)
+        turn_back(2, [1], 5, last_c[1][:].bitcast(F32), nc.scalar.copy)
         c_codes = keep.tile([P, Z], U32, name="c_codes", tag="y%d" % (L_TILES - 1), align_bytes=64)
-        for piece, z0, z1 in grouped:
+        for piece, z0, z1 in [(early_c, 0, 512), (last_c[0], 512, 640), (last_c[1], 640, 768)]:
             nc.vector.quantize_mx(out=c_codes[:, z0:z1].bitcast(FP8X4), scales=c_scales[:, z0:z1], in_=piece[:])
 
-        late = [banks[3][:, :P], banks[5][:, :P]]
-        early = [banks[0][:, :P], banks[1][:, :P]]
+        late = [banks[3][:, :P], banks[4][:, :P]]
+        early = [banks[6][:, :P], banks[7][:, :P]]
         for nh in range(2):
             for o in range(HEADS - 1):
                 merge(late[nh], nh, 1, o, o == 0, False)

@@ -20,18 +20,31 @@ MULT = mybir.AluOpType.mult
 SILU = mybir.ActivationFunctionType.Silu
 
 P = 128
+QUAD = 32
+SCALE_ROWS = 4
 L_TILES = H // P
+PASSES = HEADS
+BLOCKS = Z // P
 BANK = 512
+BANK_EXPERTS = BANK // C
 LIST_COL = 16
+
 EXPERT_GROUPS = [(0, 4), (4, 8), (8, 12), (12, 15), (15, 17), (17, 18)]
+EARLY_GROUPS = 2
 WORD_LOADS = [(0, 6), (6, 12), (12, 18)]
+LAST_PIECES = [(2, 5), (0, 1), (1, 2), (5, 6)]
+
+SUM_BANKS = [(0, 3), (1, 2), (4, 5)]
+EARLY_TURN_BANKS = [6, 7]
+LAST_TURN_BANKS = [4, 5]
+LAST_SUM_BANK = 3
 
 
 def load_scale_rows(queues, plane, rows):
-    for b in range(4):
+    for b in range(SCALE_ROWS):
         queues[b % len(queues)].dma_start(
-            out=plane[b:P:32].bitcast(I32),
-            in_=rows[:, b:16:4, :].rearrange("a q n -> q a n").bitcast(I32),
+            out=plane[b:P:QUAD].bitcast(I32),
+            in_=rows[:, b:16:SCALE_ROWS, :].rearrange("a q n -> q a n").bitcast(I32),
         )
 
 
@@ -41,7 +54,7 @@ def tile_moe_mhm_silu_kernel(
     nc = tc.nc
     with ExitStack() as ctx:
         keep = ctx.enter_context(tc.tile_pool(name="keep", bufs=1))
-        ring = ctx.enter_context(tc.tile_pool(name="ring", bufs=4))
+        ring = ctx.enter_context(tc.tile_pool(name="ring", bufs=L_TILES))
         psum = ctx.enter_context(tc.psum_pool(name="psum", bufs=1))
 
         slot_list = keep.tile([P, S // LIST_COL], U16, name="slot_list")
@@ -50,14 +63,14 @@ def tile_moe_mhm_silu_kernel(
         xs = keep.tile([P, 2 * Z], U8, name="xs", align_bytes=64)
         ww = [keep.tile([P, E, H], U8, name="ww%d" % h, align_bytes=64) for h in range(2)]
         ws = [keep.tile([P, E, H // 2], U8, name="ws%d" % h, align_bytes=64) for h in range(2)]
-        mw = keep.tile([P, HEADS, 2 * N], U8, name="mw", align_bytes=64)
-        ms = keep.tile([P, HEADS, N], U8, name="ms", align_bytes=64)
+        mw = keep.tile([P, PASSES, 2 * N], U8, name="mw", align_bytes=64)
+        ms = keep.tile([P, PASSES, N], U8, name="ms", align_bytes=64)
         gates = [keep.tile([P, Z], F32, name="gate%d" % r) for r in range(TOP)]
         y = [keep.tile([P, S], F32, name="y%d" % j, tag="y%d" % j, align_bytes=64) for j in range(L_TILES)]
-        c_rows = keep.tile([P, HEADS, 2, 2, P, 2], BF16, name="c_rows", align_bytes=64)
+        c_rows = keep.tile([P, PASSES, 2, 2, P, 2], BF16, name="c_rows", align_bytes=64)
         ident = keep.tile([P, P], F32, name="ident")
 
-        banks = [psum.tile([P, BANK], F32, name="bank%d" % b) for b in range(8)]
+        banks = [psum.tile([P, BANK], F32, name="bank%d" % k) for k in range(8)]
 
         nc.gpsimd.memset(xs[:, :Z].bitcast(I32), 0)
         nc.gpsimd.memset(xs[:, Z:].bitcast(I32), 0)
@@ -67,7 +80,6 @@ def tile_moe_mhm_silu_kernel(
         make_identity(nc, ident[:])
 
         w_words_pe = w_words.rearrange("e s p c -> p (e s) c")
-
         w_scales_eb = w_scales.rearrange("e s b l -> (e s) b l")
 
         def load_w_half(h):
@@ -92,15 +104,21 @@ def tile_moe_mhm_silu_kernel(
         load_w_half(1)
         for o in range(HEADS):
             nc.sync.dma_start(
-                out=mw[32 * o : 32 * (o + 1)].bitcast(I32),
-                in_=wm_words[o, 32:, :].rearrange("(a p) c -> p a c", p=32).bitcast(I32),
+                out=mw[QUAD * o : QUAD * (o + 1)].bitcast(I32),
+                in_=wm_words[o, QUAD:, :].rearrange("(a i) c -> i a c", i=QUAD).bitcast(I32),
             )
             nc.sync.dma_start(
-                out=ms[32 * o : 32 * o + 4].bitcast(I32),
-                in_=wm_scales[o, 4:, :].rearrange("(a b) n -> b a n", b=4).bitcast(I32),
+                out=ms[QUAD * o : QUAD * o + SCALE_ROWS].bitcast(I32),
+                in_=wm_scales[o, SCALE_ROWS:, :].rearrange("(a g) n -> g a n", g=SCALE_ROWS).bitcast(I32),
             )
-        nc.sync.dma_start(out=mw[96:].bitcast(I32), in_=wm_words[:, :32, :].rearrange("a p c -> p a c").bitcast(I32))
-        nc.sync.dma_start(out=ms[96:100].bitcast(I32), in_=wm_scales[:, :4, :].rearrange("a b n -> b a n").bitcast(I32))
+        nc.sync.dma_start(
+            out=mw[QUAD * HEADS :].bitcast(I32),
+            in_=wm_words[:, :QUAD, :].rearrange("a i c -> i a c").bitcast(I32),
+        )
+        nc.sync.dma_start(
+            out=ms[QUAD * HEADS : QUAD * HEADS + SCALE_ROWS].bitcast(I32),
+            in_=wm_scales[:, :SCALE_ROWS, :].rearrange("a g n -> g a n").bitcast(I32),
+        )
 
         slot_scales = keep.tile([P, S], U8, name="slot_scales", align_bytes=64)
         for s0 in range(0, S, S // 2):
@@ -140,96 +158,107 @@ def tile_moe_mhm_silu_kernel(
                 for b in order:
                     k, blocks = [group for group in groups if b in group[1]][0]
                     i = blocks.index(b)
+                    turns = [m for m in order if m in blocks]
                     nc.tensor.matmul(
                         banks[k][:, i * P : (i + 1) * P],
                         terms[r][:, b * P : (b + 1) * P],
                         ident[:],
-                        start=(r == 0 and i == 0),
-                        stop=(r == TOP - 1 and i == len(blocks) - 1),
+                        start=(r == 0 and b == turns[0]),
+                        stop=(r == TOP - 1 and b == turns[-1]),
                         is_transpose=True,
                     )
 
         def round_rows(j, k, blocks):
             th, heads = blocks[0] % 2, slice(blocks[0] // 2, blocks[-1] // 2 + 1)
-            sums = banks[k][:, : len(blocks) * P].rearrange("z (o q u e) -> z o u q e", u=2, e=2, q=32)
+            sums = banks[k][:, : len(blocks) * P].rearrange("t (o i u e) -> t o u i e", u=2, e=2, i=QUAD)
             if j == 0:
-                rows = c_rows[:, heads, th, :, 96:, :]
+                rows = c_rows[:, heads, th, :, QUAD * HEADS :, :]
             else:
-                rows = c_rows[:, j - 1, th].rearrange("z u (o q) e -> z o u q e", q=32)[:, heads]
+                rows = c_rows[:, j - 1, th].rearrange("t u (o i) e -> t o u i e", i=QUAD)[:, heads]
             nc.scalar.copy(rows, sums)
 
         def turn_back(a, halves, k, words, copy):
-            bank = banks[k][:, : len(halves) * 2 * P].rearrange("p (b u z) -> p b u z", u=2, z=P)
+            bank = banks[k][:, : len(halves) * 2 * P].rearrange("p (h u t) -> p h u t", u=2, t=P)
             for i, th in enumerate(halves):
                 for u in range(2):
-                    pairs = c_rows[:, a, th, u, :, :].rearrange("z p e -> z (p e)").bitcast(F32)
+                    pairs = c_rows[:, a, th, u, :, :].rearrange("t p e -> t (p e)").bitcast(F32)
                     nc.tensor.transpose(bank[:, i, u, :], pairs, ident[:])
-            copy(words.rearrange("p (b z u) -> p b z u", z=P, u=2), bank.rearrange("p b u z -> p b z u"))
+            copy(words.rearrange("p (h t u) -> p h t u", t=P, u=2), bank.rearrange("p h u t -> p h t u"))
 
         c_scales = keep.tile([P, Z], U8, name="c_scales", align_bytes=64)
 
-        def merge(sums, nh, th, o, start, stop):
-            cols = slice(o * T + th * P, o * T + (th + 1) * P)
+        def merge(sums, nh, th, a, start, stop):
+            cols = slice(a * T + th * P, a * T + (th + 1) * P)
             nc.tensor.matmul_mx(
                 out=sums,
-                lhsT=mw[:, o, 2 * P * nh : 2 * P * (nh + 1)].bitcast(FP4X4),
-                lhsT_scale=ms[:, o, P * nh : P * (nh + 1)],
+                lhsT=mw[:, a, 2 * P * nh : 2 * P * (nh + 1)].bitcast(FP4X4),
+                lhsT_scale=ms[:, a, P * nh : P * (nh + 1)],
                 rhs=c_codes[:, cols].bitcast(FP8X4),
                 rhs_scale=c_scales[:, cols],
                 start=start,
                 stop=stop,
             )
 
+        spare = banks[len(EXPERT_GROUPS) :]
         for g, (e0, e1) in enumerate(EXPERT_GROUPS):
             experts(0, e0, e1, banks[g])
             silu(0, e0, e1, banks[g])
-            if g < 2:
-                experts(1, e0, e1, banks[6 + g])
+            if g < EARLY_GROUPS:
+                experts(1, e0, e1, spare[g])
         for j in range(1, L_TILES):
-            for g, e0 in enumerate(range(0, E, 4)):
-                bank = banks[g % 4] if j == L_TILES - 1 else banks[g]
-                if j == 1 and g < 2:
-                    bank = banks[6 + g]
+            for g, e0 in enumerate(range(0, E, BANK_EXPERTS)):
+                e1 = min(e0 + BANK_EXPERTS, E)
+                if j == 1 and g < EARLY_GROUPS:
+                    bank = spare[g]
                 else:
-                    experts(j, e0, min(e0 + 4, E), bank)
-                silu(j, e0, min(e0 + 4, E), bank)
+                    bank = banks[g % 4] if j == L_TILES - 1 else banks[g]
+                    experts(j, e0, e1, bank)
+                silu(j, e0, e1, bank)
 
         early_c = keep.tile([P, 4 * 2 * T], BF16, name="early_c", align_bytes=64)
         last_c = [keep.tile([P, 4 * P], BF16, name="last_c%d" % th, align_bytes=64) for th in range(2)]
-        for j, (k0, k1) in enumerate([(0, 3), (1, 2), (4, 5)]):
-            groups = [(k0, [0, 2, 4]), (k1, [1, 3, 5])]
-            add_turned([gather(j, r, [(0, 6)]) for r in range(TOP)], groups, [0, 2, 4, 1, 3, 5])
-            for group in groups:
-                round_rows(j, *group)
+        whole = [(0, BLOCKS)]
+        half_blocks = [list(range(th, BLOCKS, 2)) for th in range(2)]
+        for j, sum_banks in enumerate(SUM_BANKS):
+            groups = list(zip(sum_banks, half_blocks))
+            add_turned([gather(j, r, whole) for r in range(TOP)], groups, half_blocks[0] + half_blocks[1])
+            for k, blocks in groups:
+                round_rows(j, k, blocks)
             if j > 0:
-                words = early_c[:].bitcast(F32)[:, (j - 1) * 2 * T : j * 2 * T]
-                turn_back(j - 1, [0, 1], 5 + j, words, nc.scalar.copy)
-        j = L_TILES - 1
-        groups = [(0, [0, 2, 4]), (1, [1, 3]), (3, [5])]
-        terms = [gather(j, 0, [(0, 6)]), gather(j, 1, [(0, 6)]), gather(j, 2, [(0, 3), (4, 5), (3, 4), (5, 6)])]
-        add_turned(terms, groups, [0, 2, 1, 4, 3, 5])
-        for group in groups:
-            round_rows(j, *group)
-        turn_back(2, [0], 4, last_c[0][:].bitcast(F32), nc.vector.tensor_copy)
-        turn_back(2, [1], 5, last_c[1][:].bitcast(F32), nc.scalar.copy)
-        c_codes = keep.tile([P, Z], U32, name="c_codes", tag="y%d" % (L_TILES - 1), align_bytes=64)
-        for piece, z0, z1 in [(early_c, 0, 512), (last_c[0], 512, 640), (last_c[1], 640, 768)]:
-            nc.vector.quantize_mx(out=c_codes[:, z0:z1].bitcast(FP8X4), scales=c_scales[:, z0:z1], in_=piece[:])
+                a = j - 1
+                words = early_c[:].bitcast(F32)[:, a * 2 * T : (a + 1) * 2 * T]
+                turn_back(a, [0, 1], EARLY_TURN_BANKS[a], words, nc.scalar.copy)
 
-        late = [banks[3][:, :P], banks[4][:, :P]]
-        early = [banks[6][:, :P], banks[7][:, :P]]
+        j, last_pass = L_TILES - 1, PASSES - 1
+        groups = [(0, [2, 4]), (2, [0]), (1, [1, 3]), (LAST_SUM_BANK, [5])]
+        terms = [gather(j, 0, whole), gather(j, 1, whole), gather(j, 2, LAST_PIECES)]
+        add_turned(terms, groups, [2, 4, 3, 0, 1, 5])
+        for k, blocks in groups:
+            round_rows(j, k, blocks)
+        for th, copy in enumerate((nc.vector.tensor_copy, nc.scalar.copy)):
+            turn_back(last_pass, [th], LAST_TURN_BANKS[th], last_c[th][:].bitcast(F32), copy)
+
+        c_codes = keep.tile([P, Z], U32, name="c_codes", tag="y%d" % (L_TILES - 1), align_bytes=64)
+        for values, c0, c1 in [(early_c, 0, 2 * T), (last_c[0], 2 * T, 2 * T + P), (last_c[1], 2 * T + P, Z)]:
+            nc.vector.quantize_mx(out=c_codes[:, c0:c1].bitcast(FP8X4), scales=c_scales[:, c0:c1], in_=values[:])
+
+        sums = [
+            [banks[k][:, :P] for k in EARLY_TURN_BANKS],
+            [banks[k][:, :P] for k in (LAST_SUM_BANK, LAST_TURN_BANKS[0])],
+        ]
         for nh in range(2):
-            for o in range(HEADS - 1):
-                merge(late[nh], nh, 1, o, o == 0, False)
+            for a in range(last_pass):
+                merge(sums[1][nh], nh, 1, a, a == 0, False)
         for nh in range(2):
-            for i, o in enumerate((2, 0, 1)):
-                merge(early[nh], nh, 0, o, i == 0, i == 2)
+            for a in (last_pass, 0, 1):
+                merge(sums[0][nh], nh, 0, a, a == last_pass, a == 1)
         for nh in range(2):
-            merge(late[nh], nh, 1, HEADS - 1, False, True)
+            merge(sums[1][nh], nh, 1, last_pass, False, True)
 
         result = keep.tile([P, 2, 2, P], F32, name="result")
-        for th, sums in enumerate((early, late)):
-            nc.scalar.copy(result[:, th, 0, :], sums[0])
-            nc.scalar.dma_start(out=out[:P, th * P : (th + 1) * P], in_=result[:, th, 0, :])
-            nc.vector.tensor_copy(result[:, th, 1, :], sums[1])
-            nc.sync.dma_start(out=out[P:, th * P : (th + 1) * P], in_=result[:, th, 1, :])
+        for th in range(2):
+            tokens = slice(th * P, (th + 1) * P)
+            nc.scalar.copy(result[:, th, 0, :], sums[th][0])
+            nc.scalar.dma_start(out=out[:P, tokens], in_=result[:, th, 0, :])
+            nc.vector.tensor_copy(result[:, th, 1, :], sums[th][1])
+            nc.sync.dma_start(out=out[P:, tokens], in_=result[:, th, 1, :])

@@ -18,6 +18,7 @@ FP8X4 = mybir.dt.float8_e4m3fn_x4
 FP4X4 = mybir.dt.float4_e2m1fn_x4
 MULT = mybir.AluOpType.mult
 SILU = mybir.ActivationFunctionType.Silu
+COPY = mybir.ActivationFunctionType.Copy
 
 P = 128
 QUAD = 32
@@ -29,15 +30,14 @@ BANK = 512
 BANK_EXPERTS = BANK // C
 LIST_COL = 16
 
-EXPERT_GROUPS = [(0, 4), (4, 8), (8, 12), (12, 15), (15, 17), (17, 18)]
-EARLY_GROUPS = 2
-WORD_LOADS = [(0, 6), (6, 12), (12, 18)]
+EXPERT_GROUPS = [(0, 4), (4, 8), (8, 12), (12, 16), (16, 18)]
+SCALE_LOADS = [(0, 4), (4, 12), (12, 18)]
 LAST_PIECES = [(2, 5), (0, 1), (1, 2), (5, 6)]
 
-SUM_BANKS = [(0, 3), (1, 2), (4, 5)]
-EARLY_TURN_BANKS = [6, 7]
-LAST_TURN_BANKS = [4, 5]
-LAST_SUM_BANK = 3
+SUM_BANKS = [(4, 5), (6, 7), (0, 1)]
+EARLY_TURN_BANKS = [2, 3]
+LAST_TURN_BANKS = [0, 1]
+LAST_SUM_BANK = 7
 
 
 def load_scale_rows(queues, plane, rows):
@@ -60,48 +60,43 @@ def tile_moe_mhm_silu_kernel(
         slot_list = keep.tile([P, S // LIST_COL], U16, name="slot_list")
         pos = [keep.tile([P, Z // LIST_COL], U16, name="pos%d" % r) for r in range(TOP)]
         xw = keep.tile([P, Z], I32, name="xw", align_bytes=64)
-        xs = keep.tile([P, 2 * Z], U8, name="xs", align_bytes=64)
-        ww = [keep.tile([P, E, H], U8, name="ww%d" % h, align_bytes=64) for h in range(2)]
-        ws = [keep.tile([P, E, H // 2], U8, name="ws%d" % h, align_bytes=64) for h in range(2)]
+        xs = keep.tile([P, Z], U8, name="xs", align_bytes=64)
+        ww = [keep.tile([P, e1 - e0, 2 * H], U8, name="ww%d" % e0, align_bytes=64) for e0, e1 in EXPERT_GROUPS]
+        ws = [keep.tile([P, e1 - e0, H], U8, name="ws%d" % e0, align_bytes=64) for e0, e1 in SCALE_LOADS]
         mw = keep.tile([P, PASSES, 2 * N], U8, name="mw", align_bytes=64)
         ms = keep.tile([P, PASSES, N], U8, name="ms", align_bytes=64)
-        gates = [keep.tile([P, Z], F32, name="gate%d" % r) for r in range(TOP)]
+        gate_rows = keep.tile([P, TOP, Z], F32, name="gate_rows")
+        gates = [gate_rows[:, r, :] for r in range(TOP)]
         y = [keep.tile([P, S], F32, name="y%d" % j, tag="y%d" % j, align_bytes=64) for j in range(L_TILES)]
         c_rows = keep.tile([P, PASSES, 2, 2, P, 2], BF16, name="c_rows", align_bytes=64)
         ident = keep.tile([P, P], F32, name="ident")
 
         banks = [psum.tile([P, BANK], F32, name="bank%d" % k) for k in range(8)]
 
-        nc.gpsimd.memset(xs[:, :Z].bitcast(I32), 0)
-        nc.gpsimd.memset(xs[:, Z:].bitcast(I32), 0)
+        nc.gpsimd.memset(xs[:].bitcast(I32), 0)
         nc.vector.memset(ws[0][:].bitcast(I32), 0)
-        nc.gpsimd.memset(ws[1][:].bitcast(I32), 0)
+        nc.vector.memset(ws[1][:].bitcast(I32), 0)
+        nc.gpsimd.memset(ws[2][:].bitcast(I32), 0)
         nc.gpsimd.memset(ms[:].bitcast(I32), 0)
         make_identity(nc, ident[:])
 
         w_words_pe = w_words.rearrange("e s p c -> p (e s) c")
         w_scales_eb = w_scales.rearrange("e s b l -> (e s) b l")
 
-        def load_w_half(h):
-            load_scale_rows([nc.sync], ws[h][:], w_scales_eb[:, :, h * H // 2 : (h + 1) * H // 2])
-            for e0, e1 in WORD_LOADS:
-                nc.sync.dma_start(
-                    out=ww[h][:, e0:e1, :].bitcast(I32),
-                    in_=w_words_pe[:, e0:e1, h * H : (h + 1) * H].bitcast(I32),
-                )
-
         nc.sync.dma_start(slot_list[:], offs)
-        load_scale_rows([nc.scalar, nc.sync], xs[:, :Z].rearrange("p (o t) -> p o t", o=HEADS), x_scales)
-        for r, pos_r in enumerate((pos1, pos2, pos3)):
-            nc.sync.dma_start(pos[r][:], pos_r)
+        load_scale_rows([nc.sync, nc.scalar, nc.scalar, nc.scalar], xs[:].rearrange("p (o t) -> p o t", o=HEADS), x_scales)
         nc.sync.dma_start(
             out=xw[:].rearrange("p (o t) -> p o t", o=HEADS),
             in_=x_words.rearrange("o p t d -> p o (t d)").bitcast(I32),
         )
-        load_w_half(0)
-        for r in range(TOP):
-            nc.sync.dma_start(out=gates[r][:], in_=gate[r])
-        load_w_half(1)
+        for i, (s0, s1) in enumerate(SCALE_LOADS):
+            load_scale_rows([nc.sync], ws[i][:], w_scales_eb[s0:s1])
+            for g, (e0, e1) in enumerate(EXPERT_GROUPS):
+                if s0 <= e0 < s1:
+                    nc.sync.dma_start(out=ww[g][:].bitcast(I32), in_=w_words_pe[:, e0:e1, :].bitcast(I32))
+        nc.sync.dma_start(out=gate_rows[:], in_=gate.rearrange("r p z -> p r z"))
+        for r, pos_r in ((2, pos3), (0, pos1), (1, pos2)):
+            nc.sync.dma_start(pos[r][:], pos_r)
         for o in range(HEADS):
             nc.sync.dma_start(
                 out=mw[QUAD * o : QUAD * (o + 1)].bitcast(I32),
@@ -121,21 +116,21 @@ def tile_moe_mhm_silu_kernel(
         )
 
         slot_scales = keep.tile([P, S], U8, name="slot_scales", align_bytes=64)
-        for s0 in range(0, S, S // 2):
-            offsets = slot_list[:, s0 // LIST_COL : (s0 + S // 2) // LIST_COL]
-            nc.vector.tensor_copy(slot_scales[:, s0 : s0 + S // 2], xs[:].indirect(offsets))
         slot_words = keep.tile([P, S], U32, name="slot_words", align_bytes=64)
         for e0, e1 in EXPERT_GROUPS:
             offsets = slot_list[:, e0 * C // LIST_COL : e1 * C // LIST_COL]
             nc.vector.tensor_copy(slot_words[:, e0 * C : e1 * C], xw[:].bitcast(U32).indirect(offsets))
+            nc.vector.tensor_copy(slot_scales[:, e0 * C : e1 * C], xs[:].indirect(offsets))
 
-        def experts(j, e0, e1, bank):
+        def experts(j, g, bank):
+            e0, e1 = EXPERT_GROUPS[g]
             for e in range(e0, e1):
+                i = [n for n, (s0, s1) in enumerate(SCALE_LOADS) if s0 <= e < s1][0]
                 cols = slice((e - e0) * C, (e - e0 + 1) * C)
                 nc.tensor.matmul_mx(
                     out=bank[:, cols],
-                    lhsT=ww[j // 2][:, e, 2 * P * (j % 2) : 2 * P * (j % 2 + 1)].bitcast(FP4X4),
-                    lhsT_scale=ws[j // 2][:, e, P * (j % 2) : P * (j % 2 + 1)],
+                    lhsT=ww[g][:, e - e0, 2 * P * j : 2 * P * (j + 1)].bitcast(FP4X4),
+                    lhsT_scale=ws[i][:, e - SCALE_LOADS[i][0], P * j : P * (j + 1)],
                     rhs=slot_words[:, e * C : (e + 1) * C].bitcast(FP8X4),
                     rhs_scale=slot_scales[:, e * C : (e + 1) * C],
                     start=True,
@@ -152,6 +147,14 @@ def tile_moe_mhm_silu_kernel(
                 offsets = pos[r][:, z0 // LIST_COL : z1 // LIST_COL]
                 nc.vector.tensor_tensor(term[:, z0:z1], y[j][:].indirect(offsets), gates[r][:, z0:z1], MULT)
             return term
+
+        def fetch(j, r):
+            term = ring.tile([P, Z], F32, name="term", tag="term%d" % r)
+            nc.scalar.activation(term[:], y[j][:].indirect(pos[r][:]), COPY)
+            return term
+
+        def weigh(term, r):
+            nc.vector.tensor_tensor(term[:], term[:], gates[r], MULT)
 
         def add_turned(terms, groups, order):
             for r in range(TOP):
@@ -199,39 +202,47 @@ def tile_moe_mhm_silu_kernel(
                 stop=stop,
             )
 
-        spare = banks[len(EXPERT_GROUPS) :]
-        for g, (e0, e1) in enumerate(EXPERT_GROUPS):
-            experts(0, e0, e1, banks[g])
-            silu(0, e0, e1, banks[g])
-            if g < EARLY_GROUPS:
-                experts(1, e0, e1, spare[g])
-        for j in range(1, L_TILES):
-            for g, e0 in enumerate(range(0, E, BANK_EXPERTS)):
-                e1 = min(e0 + BANK_EXPERTS, E)
-                if j == 1 and g < EARLY_GROUPS:
-                    bank = spare[g]
-                else:
-                    bank = banks[g % 4] if j == L_TILES - 1 else banks[g]
-                    experts(j, e0, e1, bank)
-                silu(j, e0, e1, bank)
+        steps = [(g, j) for g in range(3) for j in range(L_TILES)]
+        steps = steps + [(3, 0), (3, 1), (4, 0), (4, 1), (3, 2), (4, 2), (3, 3), (4, 3)]
+        for n, (g, j) in enumerate(steps):
+            experts(j, g, banks[n % 8])
+            silu(j, EXPERT_GROUPS[g][0], EXPERT_GROUPS[g][1], banks[n % 8])
 
         early_c = keep.tile([P, 4 * 2 * T], BF16, name="early_c", align_bytes=64)
         last_c = [keep.tile([P, 4 * P], BF16, name="last_c%d" % th, align_bytes=64) for th in range(2)]
         whole = [(0, BLOCKS)]
         half_blocks = [list(range(th, BLOCKS, 2)) for th in range(2)]
-        for j, sum_banks in enumerate(SUM_BANKS):
-            groups = list(zip(sum_banks, half_blocks))
-            add_turned([gather(j, r, whole) for r in range(TOP)], groups, half_blocks[0] + half_blocks[1])
-            for k, blocks in groups:
+        early = [list(zip(sum_banks, half_blocks)) for sum_banks in SUM_BANKS]
+        by_half = half_blocks[0] + half_blocks[1]
+
+        def finish(j):
+            for k, blocks in early[j]:
                 round_rows(j, k, blocks)
             if j > 0:
                 a = j - 1
                 words = early_c[:].bitcast(F32)[:, a * 2 * T : (a + 1) * 2 * T]
                 turn_back(a, [0, 1], EARLY_TURN_BANKS[a], words, nc.scalar.copy)
 
+        t00, t01, t02 = gather(0, 0, whole), gather(0, 1, whole), fetch(0, 2)
+        weigh(t02, 2)
+        add_turned([t00, t01, t02], early[0], by_half)
+        t12, t11, t10 = fetch(1, 2), fetch(1, 1), gather(1, 0, whole)
+        weigh(t12, 2)
+        weigh(t11, 1)
+        add_turned([t10, t12, t11], early[1], by_half)
+        finish(0)
+        t21, t22, t32, t20 = fetch(2, 1), fetch(2, 2), fetch(3, 2), gather(2, 0, whole)
+        weigh(t21, 1)
+        weigh(t22, 2)
+        t30 = gather(3, 0, whole)
+        add_turned([t20, t21, t22], early[2], by_half)
+        finish(1)
+        finish(2)
+        weigh(t32, 2)
+
         j, last_pass = L_TILES - 1, PASSES - 1
-        groups = [(0, [2, 4]), (2, [0]), (1, [1, 3]), (LAST_SUM_BANK, [5])]
-        terms = [gather(j, 0, whole), gather(j, 1, whole), gather(j, 2, LAST_PIECES)]
+        groups = [(4, [2, 4]), (6, [0]), (5, [1, 3]), (LAST_SUM_BANK, [5])]
+        terms = [t30, t32, gather(j, 1, LAST_PIECES)]
         add_turned(terms, groups, [2, 4, 3, 0, 1, 5])
         for k, blocks in groups:
             round_rows(j, k, blocks)

from contextlib import ExitStack

import concourse.mybir as mybir
from concourse.masks import make_identity

HEADS, T, E, C, H, N, TOP = 3, 256, 18, 128, 512, 256, 3
Z = HEADS * T
S = E * C
FLOPS = 2 * H * H * S + 2 * HEADS * H * N * T

F32 = mybir.dt.float32
BF16 = mybir.dt.bfloat16
I32 = mybir.dt.int32
U32 = mybir.dt.uint32
U16 = mybir.dt.uint16
U8 = mybir.dt.uint8
FP8X4 = mybir.dt.float8_e4m3fn_x4
FP4X4 = mybir.dt.float4_e2m1fn_x4
MULT = mybir.AluOpType.mult
SILU = mybir.ActivationFunctionType.Silu
COPY = mybir.ActivationFunctionType.Copy

P = 128
QUAD = 32
SCALE_ROWS = 4
L_TILES = H // P
PASSES = HEADS
BLOCKS = Z // P
BANK = 512
BANK_EXPERTS = BANK // C
LIST_COL = 16

EXPERT_GROUPS = [(0, 4), (4, 8), (8, 12), (12, 16), (16, 18)]
SCALE_LOADS = [(0, 4), (4, 12), (12, 18)]
LAST_PIECES = [(2, 5), (0, 1), (1, 2), (5, 6)]

SUM_BANKS = [(4, 5), (6, 7), (0, 1)]
EARLY_TURN_BANKS = [2, 3]
LAST_TURN_BANKS = [0, 1]
LAST_SUM_BANK = 7


def load_scale_rows(queues, plane, rows):
    for b in range(SCALE_ROWS):
        queues[b % len(queues)].dma_start(
            out=plane[b:P:QUAD].bitcast(I32),
            in_=rows[:, b:16:SCALE_ROWS, :].rearrange("a q n -> q a n").bitcast(I32),
        )


def tile_moe_mhm_silu_kernel(
    tc, x_words, x_scales, w_words, w_scales, wm_words, wm_scales, gate, offs, pos1, pos2, pos3, out
):
    nc = tc.nc
    with ExitStack() as ctx:
        keep = ctx.enter_context(tc.tile_pool(name="keep", bufs=1))
        ring = ctx.enter_context(tc.tile_pool(name="ring", bufs=L_TILES))
        psum = ctx.enter_context(tc.psum_pool(name="psum", bufs=1))

        slot_list = keep.tile([P, S // LIST_COL], U16, name="slot_list")
        pos = [keep.tile([P, Z // LIST_COL], U16, name="pos%d" % r) for r in range(TOP)]
        xw = keep.tile([P, Z], I32, name="xw", align_bytes=64)
        xs = keep.tile([P, Z], U8, name="xs", align_bytes=64)
        ww = [keep.tile([P, e1 - e0, 2 * H], U8, name="ww%d" % e0, align_bytes=64) for e0, e1 in EXPERT_GROUPS]
        ws = [keep.tile([P, e1 - e0, H], U8, name="ws%d" % e0, align_bytes=64) for e0, e1 in SCALE_LOADS]
        mw = keep.tile([P, PASSES, 2 * N], U8, name="mw", align_bytes=64)
        ms = keep.tile([P, PASSES, N], U8, name="ms", align_bytes=64)
        gate_rows = keep.tile([P, TOP, Z], F32, name="gate_rows")
        gates = [gate_rows[:, r, :] for r in range(TOP)]
        y = [keep.tile([P, S], F32, name="y%d" % j, tag="y%d" % j, align_bytes=64) for j in range(L_TILES)]
        c_rows = keep.tile([P, PASSES, 2, 2, P, 2], BF16, name="c_rows", align_bytes=64)
        ident = keep.tile([P, P], F32, name="ident")

        banks = [psum.tile([P, BANK], F32, name="bank%d" % k) for k in range(8)]

        nc.gpsimd.memset(xs[:].bitcast(I32), 0)
        nc.vector.memset(ws[0][:].bitcast(I32), 0)
        nc.vector.memset(ws[1][:].bitcast(I32), 0)
        nc.gpsimd.memset(ws[2][:].bitcast(I32), 0)
        nc.gpsimd.memset(ms[:].bitcast(I32), 0)
        make_identity(nc, ident[:])

        w_words_pe = w_words.rearrange("e s p c -> p (e s) c")
        w_scales_eb = w_scales.rearrange("e s b l -> (e s) b l")

        nc.sync.dma_start(slot_list[:], offs)
        load_scale_rows([nc.sync, nc.scalar, nc.scalar, nc.scalar], xs[:].rearrange("p (o t) -> p o t", o=HEADS), x_scales)
        nc.sync.dma_start(
            out=xw[:].rearrange("p (o t) -> p o t", o=HEADS),
            in_=x_words.rearrange("o p t d -> p o (t d)").bitcast(I32),
        )
        for i, (s0, s1) in enumerate(SCALE_LOADS):
            load_scale_rows([nc.sync], ws[i][:], w_scales_eb[s0:s1])
            for g, (e0, e1) in enumerate(EXPERT_GROUPS):
                if s0 <= e0 < s1:
                    nc.sync.dma_start(out=ww[g][:].bitcast(I32), in_=w_words_pe[:, e0:e1, :].bitcast(I32))
        nc.sync.dma_start(out=gate_rows[:], in_=gate.rearrange("r p z -> p r z"))
        for r, pos_r in ((2, pos3), (0, pos1), (1, pos2)):
            nc.sync.dma_start(pos[r][:], pos_r)
        for o in range(HEADS):
            nc.sync.dma_start(
                out=mw[QUAD * o : QUAD * (o + 1)].bitcast(I32),
                in_=wm_words[o, QUAD:, :].rearrange("(a i) c -> i a c", i=QUAD).bitcast(I32),
            )
            nc.sync.dma_start(
                out=ms[QUAD * o : QUAD * o + SCALE_ROWS].bitcast(I32),
                in_=wm_scales[o, SCALE_ROWS:, :].rearrange("(a g) n -> g a n", g=SCALE_ROWS).bitcast(I32),
            )
        nc.sync.dma_start(
            out=mw[QUAD * HEADS :].bitcast(I32),
            in_=wm_words[:, :QUAD, :].rearrange("a i c -> i a c").bitcast(I32),
        )
        nc.sync.dma_start(
            out=ms[QUAD * HEADS : QUAD * HEADS + SCALE_ROWS].bitcast(I32),
            in_=wm_scales[:, :SCALE_ROWS, :].rearrange("a g n -> g a n").bitcast(I32),
        )

        slot_scales = keep.tile([P, S], U8, name="slot_scales", align_bytes=64)
        slot_words = keep.tile([P, S], U32, name="slot_words", align_bytes=64)
        for e0, e1 in EXPERT_GROUPS:
            offsets = slot_list[:, e0 * C // LIST_COL : e1 * C // LIST_COL]
            nc.vector.tensor_copy(slot_words[:, e0 * C : e1 * C], xw[:].bitcast(U32).indirect(offsets))
            nc.vector.tensor_copy(slot_scales[:, e0 * C : e1 * C], xs[:].indirect(offsets))

        def experts(j, g, bank):
            e0, e1 = EXPERT_GROUPS[g]
            for e in range(e0, e1):
                i = [n for n, (s0, s1) in enumerate(SCALE_LOADS) if s0 <= e < s1][0]
                cols = slice((e - e0) * C, (e - e0 + 1) * C)
                nc.tensor.matmul_mx(
                    out=bank[:, cols],
                    lhsT=ww[g][:, e - e0, 2 * P * j : 2 * P * (j + 1)].bitcast(FP4X4),
                    lhsT_scale=ws[i][:, e - SCALE_LOADS[i][0], P * j : P * (j + 1)],
                    rhs=slot_words[:, e * C : (e + 1) * C].bitcast(FP8X4),
                    rhs_scale=slot_scales[:, e * C : (e + 1) * C],
                    start=True,
                    stop=True,
                )

        def silu(j, e0, e1, bank):
            nc.scalar.activation(y[j][:, e0 * C : e1 * C], bank[:, : (e1 - e0) * C], SILU)

        def gather(j, r, pieces):
            term = ring.tile([P, Z], F32, name="term", tag="term%d" % r)
            for b0, b1 in pieces:
                z0, z1 = b0 * P, b1 * P
                offsets = pos[r][:, z0 // LIST_COL : z1 // LIST_COL]
                nc.vector.tensor_tensor(term[:, z0:z1], y[j][:].indirect(offsets), gates[r][:, z0:z1], MULT)
            return term

        def fetch(j, r):
            term = ring.tile([P, Z], F32, name="term", tag="term%d" % r)
            nc.scalar.activation(term[:], y[j][:].indirect(pos[r][:]), COPY)
            return term

        def weigh(term, r):
            nc.vector.tensor_tensor(term[:], term[:], gates[r], MULT)

        def add_turned(terms, groups, order):
            for r in range(TOP):
                for b in order:
                    k, blocks = [group for group in groups if b in group[1]][0]
                    i = blocks.index(b)
                    turns = [m for m in order if m in blocks]
                    nc.tensor.matmul(
                        banks[k][:, i * P : (i + 1) * P],
                        terms[r][:, b * P : (b + 1) * P],
                        ident[:],
                        start=(r == 0 and b == turns[0]),
                        stop=(r == TOP - 1 and b == turns[-1]),
                        is_transpose=True,
                    )

        def round_rows(j, k, blocks):
            th, heads = blocks[0] % 2, slice(blocks[0] // 2, blocks[-1] // 2 + 1)
            sums = banks[k][:, : len(blocks) * P].rearrange("t (o i u e) -> t o u i e", u=2, e=2, i=QUAD)
            if j == 0:
                rows = c_rows[:, heads, th, :, QUAD * HEADS :, :]
            else:
                rows = c_rows[:, j - 1, th].rearrange("t u (o i) e -> t o u i e", i=QUAD)[:, heads]
            nc.scalar.copy(rows, sums)

        def turn_back(a, halves, k, words, copy):
            bank = banks[k][:, : len(halves) * 2 * P].rearrange("p (h u t) -> p h u t", u=2, t=P)
            for i, th in enumerate(halves):
                for u in range(2):
                    pairs = c_rows[:, a, th, u, :, :].rearrange("t p e -> t (p e)").bitcast(F32)
                    nc.tensor.transpose(bank[:, i, u, :], pairs, ident[:])
            copy(words.rearrange("p (h t u) -> p h t u", t=P, u=2), bank.rearrange("p h u t -> p h t u"))

        c_scales = keep.tile([P, Z], U8, name="c_scales", align_bytes=64)

        def merge(sums, nh, th, a, start, stop):
            cols = slice(a * T + th * P, a * T + (th + 1) * P)
            nc.tensor.matmul_mx(
                out=sums,
                lhsT=mw[:, a, 2 * P * nh : 2 * P * (nh + 1)].bitcast(FP4X4),
                lhsT_scale=ms[:, a, P * nh : P * (nh + 1)],
                rhs=c_codes[:, cols].bitcast(FP8X4),
                rhs_scale=c_scales[:, cols],
                start=start,
                stop=stop,
            )

        steps = [(g, j) for g in range(3) for j in range(L_TILES)]
        steps = steps + [(3, 0), (3, 1), (4, 0), (4, 1), (3, 2), (4, 2), (3, 3), (4, 3)]
        for n, (g, j) in enumerate(steps):
            experts(j, g, banks[n % 8])
            silu(j, EXPERT_GROUPS[g][0], EXPERT_GROUPS[g][1], banks[n % 8])

        early_c = keep.tile([P, 4 * 2 * T], BF16, name="early_c", align_bytes=64)
        last_c = [keep.tile([P, 4 * P], BF16, name="last_c%d" % th, align_bytes=64) for th in range(2)]
        whole = [(0, BLOCKS)]
        half_blocks = [list(range(th, BLOCKS, 2)) for th in range(2)]
        early = [list(zip(sum_banks, half_blocks)) for sum_banks in SUM_BANKS]
        by_half = half_blocks[0] + half_blocks[1]

        def finish(j):
            for k, blocks in early[j]:
                round_rows(j, k, blocks)
            if j > 0:
                a = j - 1
                words = early_c[:].bitcast(F32)[:, a * 2 * T : (a + 1) * 2 * T]
                turn_back(a, [0, 1], EARLY_TURN_BANKS[a], words, nc.scalar.copy)

        t00, t01, t02 = gather(0, 0, whole), gather(0, 1, whole), fetch(0, 2)
        weigh(t02, 2)
        add_turned([t00, t01, t02], early[0], by_half)
        t12, t11, t10 = fetch(1, 2), fetch(1, 1), gather(1, 0, whole)
        weigh(t12, 2)
        weigh(t11, 1)
        add_turned([t10, t12, t11], early[1], by_half)
        finish(0)
        t21, t22, t32, t20 = fetch(2, 1), fetch(2, 2), fetch(3, 2), gather(2, 0, whole)
        weigh(t21, 1)
        weigh(t22, 2)
        t30 = gather(3, 0, whole)
        add_turned([t20, t21, t22], early[2], by_half)
        finish(1)
        finish(2)
        weigh(t32, 2)

        j, last_pass = L_TILES - 1, PASSES - 1
        groups = [(4, [2, 4]), (6, [0]), (5, [1, 3]), (LAST_SUM_BANK, [5])]
        terms = [t30, t32, gather(j, 1, LAST_PIECES)]
        add_turned(terms, groups, [2, 4, 3, 0, 1, 5])
        for k, blocks in groups:
            round_rows(j, k, blocks)
        for th, copy in enumerate((nc.vector.tensor_copy, nc.scalar.copy)):
            turn_back(last_pass, [th], LAST_TURN_BANKS[th], last_c[th][:].bitcast(F32), copy)

        c_codes = keep.tile([P, Z], U32, name="c_codes", tag="y%d" % (L_TILES - 1), align_bytes=64)
        for values, c0, c1 in [(early_c, 0, 2 * T), (last_c[0], 2 * T, 2 * T + P), (last_c[1], 2 * T + P, Z)]:
            nc.vector.quantize_mx(out=c_codes[:, c0:c1].bitcast(FP8X4), scales=c_scales[:, c0:c1], in_=values[:])

        sums = [
            [banks[k][:, :P] for k in EARLY_TURN_BANKS],
            [banks[k][:, :P] for k in (LAST_SUM_BANK, LAST_TURN_BANKS[0])],
        ]
        for nh in range(2):
            for a in range(last_pass):
                merge(sums[1][nh], nh, 1, a, a == 0, False)
        for nh in range(2):
            for a in (last_pass, 0, 1):
                merge(sums[0][nh], nh, 0, a, a == last_pass, a == 1)
        for nh in range(2):
            merge(sums[1][nh], nh, 1, last_pass, False, True)

        result = keep.tile([P, 2, 2, P], F32, name="result")
        for th in range(2):
            tokens = slice(th * P, (th + 1) * P)
            nc.scalar.copy(result[:, th, 0, :], sums[th][0])
            nc.scalar.dma_start(out=out[:P, tokens], in_=result[:, th, 0, :])
            nc.vector.tensor_copy(result[:, th, 1, :], sums[th][1])
            nc.sync.dma_start(out=out[P:, tokens], in_=result[:, th, 1, :])
